import numpy as np
import ml_dtypes


def mxq(x, axis, fmt="e4m3"):
    dtype, down = {"e4m3": (ml_dtypes.float8_e4m3fn, 7), "e5m2": (ml_dtypes.float8_e5m2, 14)}[fmt]
    v = np.moveaxis(np.asarray(x, np.float32).astype(ml_dtypes.bfloat16).astype(np.float64), axis, -1)
    blocks = v.reshape(v.shape[:-1] + (-1, 32))
    amax = np.abs(blocks).max(-1, keepdims=True)
    byte = np.maximum(np.where(amax > 0, np.frexp(amax)[1] - 1 + 127, 0) - down, 1)
    scale = np.exp2(byte - 127.0)
    codes = (blocks / scale).astype(np.float32).astype(dtype).astype(np.float64)
    return np.moveaxis((codes * scale).reshape(v.shape), -1, axis)


WIDE = False


def mx_kscale(k):
    if not WIDE:
        return np.ones(k)
    levels = np.array([10, -10, 5, -5, 0])
    if k % 512:
        return np.exp2(np.random.permutation(np.resize(levels, k // 32))).repeat(32)
    a = np.empty((k // 512, 16))
    for p in range(k // 512):
        a[p, :8] = np.random.permutation(np.resize(levels, 8))
        for g in range(8):
            far = levels[np.abs(levels - a[p, g]) >= 10]
            a[p, g + 8] = far[np.random.randint(len(far))]
    return np.exp2(a.ravel()).repeat(32)


def f64(x):
    return np.asarray(x).astype(np.float64)


def striped(idx):
    return np.tile(idx.reshape(-1, 16).T, (8, 1)).astype(np.uint16)


def unstriped(offs):
    return offs[:16].T.reshape(-1).astype(np.int64)


E2M1 = np.array([0.0, 0.5, 1.0, 1.5, 2.0, 3.0, 4.0, 6.0, -0.0, -0.5, -1.0, -1.5, -2.0, -3.0, -4.0, -6.0])


def pack_fp4(w):
    k, n = w.shape
    w = f64(np.asarray(w, np.float32).astype(ml_dtypes.bfloat16)).reshape(k // 32, 32, n)
    amax = np.abs(w).max(1)
    mant, ex = np.frexp(amax / 6.0)
    byte = np.clip(np.where(amax > 0, np.where(mant > 0.5, ex, ex - 1) + 127, 1), 1, 254)
    scaled = (w * np.exp2(127.0 - byte)[:, None, :]).reshape(k, n).astype(np.float32)
    c = np.ascontiguousarray(scaled.reshape(k // 512, 128, 4, n).transpose(0, 1, 3, 2)).astype(ml_dtypes.float4_e2m1fn).view(np.uint8) & 0xF
    words = (c[..., 0::2] | (c[..., 1::2] << 4)).reshape(k // 512, 128, 2 * n)
    return np.ascontiguousarray(words), np.ascontiguousarray(byte.astype(np.uint8).reshape(k // 512, 16, n))


def unpack_fp4(words, scales):
    g, _, n = scales.shape
    words = np.ascontiguousarray(words).reshape(g, 128, n, 2)
    nib = np.empty((g, 128, n, 4), np.uint8)
    nib[..., 0::2] = words & 0xF
    nib[..., 1::2] = words >> 4
    vals = E2M1[nib] * np.repeat(np.exp2(scales.astype(np.float64) - 127.0), 8, axis=1)[..., None]
    return vals.transpose(0, 1, 3, 2).reshape(g * 512, n)


K, T, S, N, U = 512, 4096, 1024, 256, 2048
P = 2 ** 7


def setup_inputs():
    n = np.random.standard_normal
    s = mx_kscale(K)[:, None]
    packed_w1 = pack_fp4(n((K, N)) / np.sqrt(K) / s)
    return {
        "xT": (n((K, T)) * s).astype(np.float32),
        "gate": np.tile(np.random.uniform(0.5, 1.5, S), (P, 1)).astype(np.float32),
        "w1_words": packed_w1[0],
        "w1_scales": packed_w1[1],
        "offs": striped(np.random.permutation(T)[:S]),
        "dst": striped(np.random.permutation(U)[:S]),
    }


def reference(xT, gate, w1_words, w1_scales, offs, dst):
    xq = mxq(f64(xT)[:, unstriped(offs)], 0, "e4m3")
    y = unpack_fp4(w1_words, w1_scales).T @ xq
    out = np.zeros((N, U))
    out[:, unstriped(dst)] = y * f64(gate)[:1]
    return out

@@ -1,0 +1,126 @@
+from contextlib import ExitStack
+
+import concourse.mybir as mybir
+
+K, T, S, N, U = 512, 4096, 1024, 256, 2048
+FLOPS = 2 * K * N * S
+
+F32 = mybir.dt.float32
+BF16 = mybir.dt.bfloat16
+I32 = mybir.dt.int32
+U32 = mybir.dt.uint32
+U16 = mybir.dt.uint16
+U8 = mybir.dt.uint8
+FP8X4 = mybir.dt.float8_e4m3fn_x4
+FP4X4 = mybir.dt.float4_e2m1fn_x4
+COPY = mybir.ActivationFunctionType.Copy
+MULT = mybir.AluOpType.mult
+
+P = 128
+PACK = 4
+STRIPE = 16
+HALF = S // 2
+LEAD = 256
+LAST_PLANE_CHUNKS = ((1280, "scalar"), (1024, "scalar"), (1024, "vector"), (768, "scalar"))
+
+
+def tile_picked_route2_linnone_e_kernel(tc, xT, gate, w1_words, w1_scales, offs, dst, out):
+    nc = tc.nc
+    x_planes = xT.rearrange("(p j) t -> p j t", j=PACK)
+
+    with ExitStack() as ctx:
+        keep = ctx.enter_context(tc.tile_pool(name="keep", bufs=1))
+        psum = ctx.enter_context(tc.psum_pool(name="psum", bufs=1))
+
+        pick = keep.tile([P, S // STRIPE], U16, name="pick")
+        place = keep.tile([P, S // STRIPE], U16, name="place")
+        plane = [keep.tile([P, T], F32, name=f"plane{j}") for j in range(PACK)]
+        plane_bf16 = {j: keep.tile([P, T], BF16, name=f"plane_bf16_{j}") for j in (2, 3)}
+        picked = [keep.tile([P, HALF, PACK], BF16, name=f"picked{h}", align_bytes=64) for h in range(2)]
+        codes = [keep.tile([P, HALF], U32, name=f"codes{h}", align_bytes=64) for h in range(2)]
+        scales = [keep.tile([P, HALF], U8, name=f"scales{h}", align_bytes=64) for h in range(2)]
+        w_codes = keep.tile([P, 2 * N], U8, name="w_codes", align_bytes=64)
+        w_scales = keep.tile([P, N], U8, name="w_scales", align_bytes=64)
+        gate_sb = keep.tile([P, S], F32, name="gate_sb")
+        y = [keep.tile([P, S], F32, name=f"y{b}") for b in range(2)]
+        window = [keep.tile([P, U], F32, name=f"window{b}") for b in range(2)]
+
+        def entries(list_tile, start, stop):
+            return list_tile[:, start // STRIPE : stop // STRIPE]
+
+        nc.sync.dma_start(out=plane[2][:], in_=x_planes[:, 2, :])
+        nc.sync.dma_start(pick[:], offs)
+        nc.sync.dma_start(out=plane[0][:], in_=x_planes[:, 0, :])
+        nc.sync.dma_start(out=plane[1][:], in_=x_planes[:, 1, :])
+        start = 0
+        for width, engine in LAST_PLANE_CHUNKS:
+            nc.sync.dma_start(out=plane[3][:, start : start + width], in_=x_planes[:, 3, start : start + width])
+            start += width
+        nc.sync.dma_start(out=w_codes[:].bitcast(I32), in_=w1_words[0].bitcast(I32))
+        nc.sync.dma_start(place[:], dst)
+        nc.sync.dma_start(out=gate_sb[:], in_=gate)
+
+        nc.gpsimd.memset(w_scales[:], 0)
+        for q in range(4):
+            nc.gpsimd.dma_start(
+                out=w_scales[32 * q : 32 * q + 4, :].bitcast(I32),
+                in_=w1_scales[0, 4 * q : 4 * q + 4, :].bitcast(I32),
+            )
+        for b in range(2):
+            nc.vector.memset(window[b][:], 0.0)
+
+        def gather_on_vector(j, h):
+            nc.vector.tensor_copy(picked[h][:, :, j], plane[j][:].indirect(entries(pick, h * HALF, (h + 1) * HALF)))
+
+        def gather_on_scalar(j, h):
+            nc.scalar.activation(picked[h][:, :, j], plane_bf16[j][:].indirect(entries(pick, h * HALF, (h + 1) * HALF)), COPY)
+
+        gather_on_vector(2, 0)
+        nc.scalar.activation(plane_bf16[2][:], plane[2][:], COPY)
+        gather_on_scalar(2, 1)
+        for j in (0, 1):
+            gather_on_vector(j, 0)
+            gather_on_vector(j, 1)
+        start = 0
+        for width, engine in LAST_PLANE_CHUNKS:
+            cols = slice(start, start + width)
+            if engine == "scalar":
+                nc.scalar.activation(plane_bf16[3][:, cols], plane[3][:, cols], COPY)
+            else:
+                nc.vector.tensor_copy(plane_bf16[3][:, cols], plane[3][:, cols])
+            start += width
+        gather_on_vector(3, 0)
+        gather_on_scalar(3, 1)
+
+        def product(start, stop):
+            h, first = divmod(start, HALF)
+            cols = slice(first, first + stop - start)
+            nc.vector.quantize_mx(
+                out=codes[h][:, cols].bitcast(FP8X4),
+                scales=scales[h][:, cols],
+                in_=picked[h][:, cols, :].rearrange("p n j -> p (n j)"),
+            )
+            for b in range(2):
+                acc = psum.tile([P, stop - start], F32, name=f"acc{start}_{b}")
+                nc.tensor.matmul_mx(
+                    out=acc[:],
+                    lhsT=w_codes[:, 2 * P * b : 2 * P * (b + 1)].bitcast(FP4X4),
+                    lhsT_scale=w_scales[:, P * b : P * (b + 1)],
+                    rhs=codes[h][:, cols].bitcast(FP8X4),
+                    rhs_scale=scales[h][:, cols],
+                    start=True,
+                    stop=True,
+                )
+                nc.scalar.activation(y[b][:, start:stop], acc[:], COPY)
+
+        product(0, LEAD)
+        product(LEAD, HALF)
+        product(HALF, S)
+
+        for start, stop in ((0, LEAD), (LEAD, S)):
+            for b in range(2):
+                nc.vector.tensor_tensor(
+                    window[b][:].indirect(entries(place, start, stop)), y[b][:, start:stop], gate_sb[:, start:stop], MULT
+                )
+        for b in range(2):
+            nc.sync.dma_start(out=out[P * b : P * (b + 1), :], in_=window[b][:])

@@ -21,7 +21,7 @@ PACK = 4
 STRIPE = 16
 HALF = S // 2
 LEAD = 256
-LAST_PLANE_CHUNKS = ((1280, "scalar"), (1024, "scalar"), (1024, "vector"), (768, "scalar"))
+LAST_PLANE_CHUNKS = ((1280, 768), (640, 768), (640, 0))
 
 
 def tile_picked_route2_linnone_e_kernel(tc, xT, gate, w1_words, w1_scales, offs, dst, out):
@@ -53,19 +53,20 @@ def tile_picked_route2_linnone_e_kernel(tc, xT, gate, w1_words, w1_scales, offs,
         nc.sync.dma_start(out=plane[0][:], in_=x_planes[:, 0, :])
         nc.sync.dma_start(out=plane[1][:], in_=x_planes[:, 1, :])
         start = 0
-        for width, engine in LAST_PLANE_CHUNKS:
-            nc.sync.dma_start(out=plane[3][:, start : start + width], in_=x_planes[:, 3, start : start + width])
-            start += width
+        for on_scalar, on_vector in LAST_PLANE_CHUNKS:
+            cols = slice(start, start + on_scalar + on_vector)
+            nc.sync.dma_start(out=plane[3][:, cols], in_=x_planes[:, 3, cols])
+            start = cols.stop
         nc.sync.dma_start(out=w_codes[:].bitcast(I32), in_=w1_words[0].bitcast(I32))
-        nc.sync.dma_start(place[:], dst)
-        nc.sync.dma_start(out=gate_sb[:], in_=gate)
-
-        nc.gpsimd.memset(w_scales[:], 0)
+        nc.vector.memset(w_scales[:].bitcast(I32), 0)
         for q in range(4):
-            nc.gpsimd.dma_start(
+            nc.sync.dma_start(
                 out=w_scales[32 * q : 32 * q + 4, :].bitcast(I32),
                 in_=w1_scales[0, 4 * q : 4 * q + 4, :].bitcast(I32),
             )
+        nc.sync.dma_start(place[:], dst)
+        nc.sync.dma_start(out=gate_sb[:], in_=gate)
+
         for b in range(2):
             nc.vector.memset(window[b][:], 0.0)
 
@@ -82,17 +83,18 @@ def tile_picked_route2_linnone_e_kernel(tc, xT, gate, w1_words, w1_scales, offs,
             gather_on_vector(j, 0)
             gather_on_vector(j, 1)
         start = 0
-        for width, engine in LAST_PLANE_CHUNKS:
-            cols = slice(start, start + width)
-            if engine == "scalar":
-                nc.scalar.activation(plane_bf16[3][:, cols], plane[3][:, cols], COPY)
-            else:
+        for on_scalar, on_vector in LAST_PLANE_CHUNKS:
+            cols = slice(start, start + on_scalar)
+            nc.scalar.activation(plane_bf16[3][:, cols], plane[3][:, cols], COPY)
+            start = cols.stop
+            if on_vector:
+                cols = slice(start, start + on_vector)
                 nc.vector.tensor_copy(plane_bf16[3][:, cols], plane[3][:, cols])
-            start += width
+                start = cols.stop
         gather_on_vector(3, 0)
         gather_on_scalar(3, 1)
 
-        def product(start, stop):
+        def quantise(start, stop):
             h, first = divmod(start, HALF)
             cols = slice(first, first + stop - start)
             nc.vector.quantize_mx(
@@ -100,22 +102,30 @@ def tile_picked_route2_linnone_e_kernel(tc, xT, gate, w1_words, w1_scales, offs,
                 scales=scales[h][:, cols],
                 in_=picked[h][:, cols, :].rearrange("p n j -> p (n j)"),
             )
-            for b in range(2):
-                acc = psum.tile([P, stop - start], F32, name=f"acc{start}_{b}")
-                nc.tensor.matmul_mx(
-                    out=acc[:],
-                    lhsT=w_codes[:, 2 * P * b : 2 * P * (b + 1)].bitcast(FP4X4),
-                    lhsT_scale=w_scales[:, P * b : P * (b + 1)],
-                    rhs=codes[h][:, cols].bitcast(FP8X4),
-                    rhs_scale=scales[h][:, cols],
-                    start=True,
-                    stop=True,
-                )
-                nc.scalar.activation(y[b][:, start:stop], acc[:], COPY)
 
-        product(0, LEAD)
-        product(LEAD, HALF)
-        product(HALF, S)
+        def product(b, start, stop):
+            h, first = divmod(start, HALF)
+            cols = slice(first, first + stop - start)
+            acc = psum.tile([P, stop - start], F32, name=f"acc{start}_{b}")
+            nc.tensor.matmul_mx(
+                out=acc[:],
+                lhsT=w_codes[:, 2 * P * b : 2 * P * (b + 1)].bitcast(FP4X4),
+                lhsT_scale=w_scales[:, P * b : P * (b + 1)],
+                rhs=codes[h][:, cols].bitcast(FP8X4),
+                rhs_scale=scales[h][:, cols],
+                start=True,
+                stop=True,
+            )
+            nc.scalar.activation(y[b][:, start:stop], acc[:], COPY)
+
+        for start in (0, LEAD // 2):
+            quantise(start, start + LEAD // 2)
+            product(0, start, start + LEAD // 2)
+        product(1, 0, LEAD)
+        for start, stop in ((LEAD, HALF), (HALF, S)):
+            quantise(start, stop)
+            for b in range(2):
+                product(b, start, stop)
 
         for start, stop in ((0, LEAD), (LEAD, S)):
             for b in range(2):

@@ -50,6 +50,12 @@ def tile_picked_route2_linnone_e_kernel(tc, xT, gate, w1_words, w1_scales, offs,
 
         nc.sync.dma_start(out=plane[2][:], in_=x_planes[:, 2, :])
         nc.sync.dma_start(pick[:], offs)
+        nc.vector.memset(w_scales[:].bitcast(I32), 0)
+        for q in range(4):
+            nc.sync.dma_start(
+                out=w_scales[32 * q : 32 * q + 4, :].bitcast(I32),
+                in_=w1_scales[0, 4 * q : 4 * q + 4, :].bitcast(I32),
+            )
         nc.sync.dma_start(out=plane[0][:], in_=x_planes[:, 0, :])
         nc.sync.dma_start(out=plane[1][:], in_=x_planes[:, 1, :])
         start = 0
@@ -58,12 +64,6 @@ def tile_picked_route2_linnone_e_kernel(tc, xT, gate, w1_words, w1_scales, offs,
             nc.sync.dma_start(out=plane[3][:, cols], in_=x_planes[:, 3, cols])
             start = cols.stop
         nc.sync.dma_start(out=w_codes[:].bitcast(I32), in_=w1_words[0].bitcast(I32))
-        nc.vector.memset(w_scales[:].bitcast(I32), 0)
-        for q in range(4):
-            nc.sync.dma_start(
-                out=w_scales[32 * q : 32 * q + 4, :].bitcast(I32),
-                in_=w1_scales[0, 4 * q : 4 * q + 4, :].bitcast(I32),
-            )
         nc.sync.dma_start(place[:], dst)
         nc.sync.dma_start(out=gate_sb[:], in_=gate)
 

@@ -19,9 +19,14 @@ MULT = mybir.AluOpType.mult
 P = 128
 PACK = 4
 STRIPE = 16
-HALF = S // 2
-LEAD = 256
-LAST_PLANE_CHUNKS = ((1280, 768), (640, 768), (640, 0))
+ALIGN = 256
+PIECE = 128
+LEAD = 2 * PIECE
+ON_VECTOR = 2 * PIECE
+STEPPED = 512
+LATE = ON_VECTOR + STEPPED
+WIDE = 512
+LAST_PLANE_CHUNKS = ((1536, 0), (704, 832), (256, 512), (256, 0))
 
 
 def tile_picked_route2_linnone_e_kernel(tc, xT, gate, w1_words, w1_scales, offs, dst, out):
@@ -32,18 +37,24 @@ def tile_picked_route2_linnone_e_kernel(tc, xT, gate, w1_words, w1_scales, offs,
         keep = ctx.enter_context(tc.tile_pool(name="keep", bufs=1))
         psum = ctx.enter_context(tc.psum_pool(name="psum", bufs=1))
 
-        pick = keep.tile([P, S // STRIPE], U16, name="pick")
-        place = keep.tile([P, S // STRIPE], U16, name="place")
-        plane = [keep.tile([P, T], F32, name=f"plane{j}") for j in range(PACK)]
-        plane_bf16 = {j: keep.tile([P, T], BF16, name=f"plane_bf16_{j}") for j in (2, 3)}
-        picked = [keep.tile([P, HALF, PACK], BF16, name=f"picked{h}", align_bytes=64) for h in range(2)]
-        codes = [keep.tile([P, HALF], U32, name=f"codes{h}", align_bytes=64) for h in range(2)]
-        scales = [keep.tile([P, HALF], U8, name=f"scales{h}", align_bytes=64) for h in range(2)]
-        w_codes = keep.tile([P, 2 * N], U8, name="w_codes", align_bytes=64)
-        w_scales = keep.tile([P, N], U8, name="w_scales", align_bytes=64)
-        gate_sb = keep.tile([P, S], F32, name="gate_sb")
-        y = [keep.tile([P, S], F32, name=f"y{b}") for b in range(2)]
-        window = [keep.tile([P, U], F32, name=f"window{b}") for b in range(2)]
+        def tile(name, shape, dtype, tag=None):
+            return keep.tile(shape, dtype, name=name, tag=tag or name, align_bytes=ALIGN)
+
+        pick = tile("pick", [P, S // STRIPE], U16)
+        place = tile("place", [P, S // STRIPE], U16)
+        plane = [tile(f"plane{j}", [P, T], F32) for j in range(PACK)]
+        plane_bf16 = {j: tile(f"plane_bf16_{j}", [P, T], BF16) for j in (2, 3)}
+        picked = tile("picked", [P, S, PACK], BF16)
+        lead_codes = tile("lead_codes", [P, LEAD], U32, tag="relay")
+        rest_codes = tile("rest_codes", [P, LATE - LEAD], U32)
+        lead_scales = tile("lead_scales", [P, LEAD], U8)
+        rest_scales = tile("rest_scales", [P, LATE - LEAD], U8)
+        late_scales = tile("late_scales", [P, S - LATE], U8)
+        late_codes = []
+        w_codes = tile("w_codes", [P, 2 * N], U8)
+        w_scales = tile("w_scales", [P, N], U8)
+        gate_sb = tile("gate_sb", [P, S], F32)
+        window = [tile(f"window{b}", [P, U], F32) for b in range(2)]
 
         def entries(list_tile, start, stop):
             return list_tile[:, start // STRIPE : stop // STRIPE]
@@ -63,25 +74,26 @@ def tile_picked_route2_linnone_e_kernel(tc, xT, gate, w1_words, w1_scales, offs,
             cols = slice(start, start + on_scalar + on_vector)
             nc.sync.dma_start(out=plane[3][:, cols], in_=x_planes[:, 3, cols])
             start = cols.stop
-        nc.sync.dma_start(out=w_codes[:].bitcast(I32), in_=w1_words[0].bitcast(I32))
+        for b in range(2):
+            cols = slice(2 * P * b, 2 * P * (b + 1))
+            nc.sync.dma_start(out=w_codes[:, cols].bitcast(I32), in_=w1_words[0][:, cols].bitcast(I32))
         nc.sync.dma_start(place[:], dst)
-        nc.sync.dma_start(out=gate_sb[:], in_=gate)
+        for start in range(0, S, LEAD):
+            nc.sync.dma_start(out=gate_sb[:, start : start + LEAD], in_=gate[:, start : start + LEAD])
 
         for b in range(2):
             nc.vector.memset(window[b][:], 0.0)
 
-        def gather_on_vector(j, h):
-            nc.vector.tensor_copy(picked[h][:, :, j], plane[j][:].indirect(entries(pick, h * HALF, (h + 1) * HALF)))
+        def looked_up(table, start, stop):
+            return table[:].indirect(entries(pick, start, stop))
 
-        def gather_on_scalar(j, h):
-            nc.scalar.activation(picked[h][:, :, j], plane_bf16[j][:].indirect(entries(pick, h * HALF, (h + 1) * HALF)), COPY)
-
-        gather_on_vector(2, 0)
+        plain2 = tile("plain2", [P, ON_VECTOR], BF16)
+        nc.vector.tensor_copy(plain2[:], looked_up(plane[2], 0, ON_VECTOR))
+        nc.vector.tensor_copy(picked[:, 0:ON_VECTOR, 2], plain2[:])
         nc.scalar.activation(plane_bf16[2][:], plane[2][:], COPY)
-        gather_on_scalar(2, 1)
+        nc.scalar.activation(picked[:, ON_VECTOR:S, 2], looked_up(plane_bf16[2], ON_VECTOR, S), COPY)
         for j in (0, 1):
-            gather_on_vector(j, 0)
-            gather_on_vector(j, 1)
+            nc.vector.tensor_copy(picked[:, :, j], looked_up(plane[j], 0, S))
         start = 0
         for on_scalar, on_vector in LAST_PLANE_CHUNKS:
             cols = slice(start, start + on_scalar)
@@ -91,46 +103,83 @@ def tile_picked_route2_linnone_e_kernel(tc, xT, gate, w1_words, w1_scales, offs,
                 cols = slice(start, start + on_vector)
                 nc.vector.tensor_copy(plane_bf16[3][:, cols], plane[3][:, cols])
                 start = cols.stop
-        gather_on_vector(3, 0)
-        gather_on_scalar(3, 1)
+
+        def fetch_piece(i):
+            plain = tile(f"plain3_{i}", [P, PIECE], BF16, tag=f"plain3_{i % 2}")
+            nc.vector.tensor_copy(plain[:], looked_up(plane[3], i * PIECE, (i + 1) * PIECE))
+            return plain
+
+        def weave_piece(i, plain):
+            nc.vector.tensor_copy(picked[:, i * PIECE : (i + 1) * PIECE, 3], plain[:])
+
+        def operand(start, stop):
+            if stop <= LEAD:
+                return lead_codes[:, start:stop].bitcast(FP8X4), lead_scales[:, start:stop]
+            if start >= LATE:
+                return late_codes[0][:].bitcast(FP8X4), late_scales[:]
+            return rest_codes[:, start - LEAD : stop - LEAD].bitcast(FP8X4), rest_scales[:, start - LEAD : stop - LEAD]
 
         def quantise(start, stop):
-            h, first = divmod(start, HALF)
-            cols = slice(first, first + stop - start)
-            nc.vector.quantize_mx(
-                out=codes[h][:, cols].bitcast(FP8X4),
-                scales=scales[h][:, cols],
-                in_=picked[h][:, cols, :].rearrange("p n j -> p (n j)"),
-            )
+            codes, scales = operand(start, stop)
+            nc.vector.quantize_mx(out=codes, scales=scales, in_=picked[:, start:stop, :].rearrange("p n j -> p (n j)"))
 
-        def product(b, start, stop):
-            h, first = divmod(start, HALF)
-            cols = slice(first, first + stop - start)
-            acc = psum.tile([P, stop - start], F32, name=f"acc{start}_{b}")
+        def bank(b, start, stop):
+            return psum.tile([P, stop - start], F32, name=f"acc{start}_{b}")
+
+        def product(acc, b, start, stop):
+            codes, scales = operand(start, stop)
             nc.tensor.matmul_mx(
-                out=acc[:],
+                out=acc,
                 lhsT=w_codes[:, 2 * P * b : 2 * P * (b + 1)].bitcast(FP4X4),
                 lhsT_scale=w_scales[:, P * b : P * (b + 1)],
-                rhs=codes[h][:, cols].bitcast(FP8X4),
-                rhs_scale=scales[h][:, cols],
+                rhs=codes,
+                rhs_scale=scales,
                 start=True,
                 stop=True,
             )
-            nc.scalar.activation(y[b][:, start:stop], acc[:], COPY)
 
-        for start in (0, LEAD // 2):
-            quantise(start, start + LEAD // 2)
-            product(0, start, start + LEAD // 2)
-        product(1, 0, LEAD)
-        for start, stop in ((LEAD, HALF), (HALF, S)):
-            quantise(start, stop)
-            for b in range(2):
-                product(b, start, stop)
+        def scatter(b, start, stop, values):
+            nc.vector.tensor_tensor(window[b][:].indirect(entries(place, start, stop)), values, gate_sb[:, start:stop], MULT)
 
-        for start, stop in ((0, LEAD), (LEAD, S)):
-            for b in range(2):
-                nc.vector.tensor_tensor(
-                    window[b][:].indirect(entries(place, start, stop)), y[b][:, start:stop], gate_sb[:, start:stop], MULT
-                )
+        nc.scalar.activation(picked[:, ON_VECTOR:LATE, 3], looked_up(plane_bf16[3], ON_VECTOR, LATE), COPY)
+        first, second = fetch_piece(0), fetch_piece(1)
+        weave_piece(0, first)
+        weave_piece(1, second)
+        lead_y = [tile("lead_y0", [P, LEAD], F32, tag="after_first_scatter"), tile("lead_y1", [P, LEAD], F32)]
+        for start in (0, PIECE):
+            quantise(start, start + PIECE)
+            acc = bank(0, start, start + PIECE)
+            product(acc[:], 0, start, start + PIECE)
+            nc.scalar.activation(lead_y[0][:, start : start + PIECE], acc[:], COPY)
+        acc = bank(1, 0, LEAD)
+        product(acc[:], 1, 0, LEAD)
+        nc.scalar.activation(lead_y[1][:], acc[:], COPY)
+        quantise(ON_VECTOR, LATE)
+
+        late_plain = tile("late_plain", [P, S - LATE], BF16, tag="relay")
+        nc.scalar.activation(late_plain[:], looked_up(plane_bf16[3], LATE, S), COPY)
+        nc.scalar.activation(picked[:, LATE:S, 3], late_plain[:], COPY)
+
+        rest_y = [tile(f"rest_y{b}", [P, S - LEAD], F32) for b in range(2)]
+        mid = LEAD + WIDE
         for b in range(2):
-            nc.sync.dma_start(out=out[P * b : P * (b + 1), :], in_=window[b][:])
+            acc = bank(b, LEAD, mid)
+            product(acc[:], b, LEAD, mid)
+            nc.scalar.activation(rest_y[b][:, 0:WIDE], acc[:], COPY)
+
+        for b in range(2):
+            scatter(b, 0, LEAD, lead_y[b][:])
+        late_codes.append(tile("late_codes", [P, S - LATE], U32, tag="after_first_scatter"))
+        quantise(LATE, S)
+        for b in range(2):
+            acc = bank(b, mid, S)
+            product(acc[:, LATE - mid :], b, LATE, S)
+            nc.scalar.activation(rest_y[b][:, WIDE:], acc[:], COPY)
+
+        scatter(0, LEAD, mid, rest_y[0][:, 0:WIDE])
+        scatter(1, LEAD, 2 * LEAD, rest_y[1][:, 0:LEAD])
+        scatter(0, mid, S, rest_y[0][:, WIDE:])
+        for start in range(0, U, U // 4):
+            nc.sync.dma_start(out=out[0:P, start : start + U // 4], in_=window[0][:, start : start + U // 4])
+        scatter(1, 2 * LEAD, S, rest_y[1][:, LEAD:])
+        nc.sync.dma_start(out=out[P : 2 * P, :], in_=window[1][:])

@@ -21,12 +21,16 @@ PACK = 4
 STRIPE = 16
 ALIGN = 256
 PIECE = 128
-LEAD = 2 * PIECE
-ON_VECTOR = 2 * PIECE
-STEPPED = 512
-LATE = ON_VECTOR + STEPPED
-WIDE = 512
-LAST_PLANE_CHUNKS = ((1536, 0), (704, 832), (256, 512), (256, 0))
+LEAD = slice(0, 2 * PIECE)
+WIDE = slice(LEAD.stop, LEAD.stop + 512)
+FILL = slice(WIDE.stop, WIDE.stop + PIECE)
+LATE = slice(FILL.stop, S)
+TAIL = slice(FILL.start, S)
+LAST_PLANE_CHUNKS = ((1344, 448), (512, 1024), (160, 416), (192, 0))
+
+
+def width(part):
+    return part.stop - part.start
 
 
 def tile_picked_route2_linnone_e_kernel(tc, xT, gate, w1_words, w1_scales, offs, dst, out):
@@ -45,19 +49,13 @@ def tile_picked_route2_linnone_e_kernel(tc, xT, gate, w1_words, w1_scales, offs,
         plane = [tile(f"plane{j}", [P, T], F32) for j in range(PACK)]
         plane_bf16 = {j: tile(f"plane_bf16_{j}", [P, T], BF16) for j in (2, 3)}
         picked = tile("picked", [P, S, PACK], BF16)
-        lead_codes = tile("lead_codes", [P, LEAD], U32, tag="relay")
-        rest_codes = tile("rest_codes", [P, LATE - LEAD], U32)
-        lead_scales = tile("lead_scales", [P, LEAD], U8)
-        rest_scales = tile("rest_scales", [P, LATE - LEAD], U8)
-        late_scales = tile("late_scales", [P, S - LATE], U8)
-        late_codes = []
         w_codes = tile("w_codes", [P, 2 * N], U8)
         w_scales = tile("w_scales", [P, N], U8)
         gate_sb = tile("gate_sb", [P, S], F32)
         window = [tile(f"window{b}", [P, U], F32) for b in range(2)]
 
-        def entries(list_tile, start, stop):
-            return list_tile[:, start // STRIPE : stop // STRIPE]
+        def entries(list_tile, part):
+            return list_tile[:, part.start // STRIPE : part.stop // STRIPE]
 
         nc.sync.dma_start(out=plane[2][:], in_=x_planes[:, 2, :])
         nc.sync.dma_start(pick[:], offs)
@@ -78,22 +76,36 @@ def tile_picked_route2_linnone_e_kernel(tc, xT, gate, w1_words, w1_scales, offs,
             cols = slice(2 * P * b, 2 * P * (b + 1))
             nc.sync.dma_start(out=w_codes[:, cols].bitcast(I32), in_=w1_words[0][:, cols].bitcast(I32))
         nc.sync.dma_start(place[:], dst)
-        for start in range(0, S, LEAD):
-            nc.sync.dma_start(out=gate_sb[:, start : start + LEAD], in_=gate[:, start : start + LEAD])
+        for start in range(0, S, width(LEAD)):
+            cols = slice(start, start + width(LEAD))
+            nc.sync.dma_start(out=gate_sb[:, cols], in_=gate[:, cols])
 
         for b in range(2):
             nc.vector.memset(window[b][:], 0.0)
 
-        def looked_up(table, start, stop):
-            return table[:].indirect(entries(pick, start, stop))
+        def fetch_on_vector(j, part, tag=None):
+            plain = tile(f"plain{j}_{part.start}", [P, width(part)], BF16, tag)
+            nc.vector.tensor_copy(plain[:], plane[j][:].indirect(entries(pick, part)))
+            return plain
 
-        plain2 = tile("plain2", [P, ON_VECTOR], BF16)
-        nc.vector.tensor_copy(plain2[:], looked_up(plane[2], 0, ON_VECTOR))
-        nc.vector.tensor_copy(picked[:, 0:ON_VECTOR, 2], plain2[:])
+        def weave_on_vector(j, part, plain):
+            nc.vector.tensor_copy(picked[:, part, j], plain[:])
+
+        def stepped_on_scalar(j, part):
+            nc.scalar.activation(picked[:, part, j], plane_bf16[j][:].indirect(entries(pick, part)), COPY)
+
+        def fetch_and_weave_on_scalar(j, part, tag=None):
+            plain = tile(f"plain{j}_{part.start}", [P, width(part)], BF16, tag)
+            nc.scalar.activation(plain[:], plane_bf16[j][:].indirect(entries(pick, part)), COPY)
+            nc.scalar.activation(picked[:, part, j], plain[:], COPY)
+
+        for part in (LEAD, FILL):
+            weave_on_vector(2, part, fetch_on_vector(2, part))
         nc.scalar.activation(plane_bf16[2][:], plane[2][:], COPY)
-        nc.scalar.activation(picked[:, ON_VECTOR:S, 2], looked_up(plane_bf16[2], ON_VECTOR, S), COPY)
+        stepped_on_scalar(2, WIDE)
+        fetch_and_weave_on_scalar(2, LATE)
         for j in (0, 1):
-            nc.vector.tensor_copy(picked[:, :, j], looked_up(plane[j], 0, S))
+            nc.vector.tensor_copy(picked[:, :, j], plane[j][:].indirect(pick[:]))
         start = 0
         for on_scalar, on_vector in LAST_PLANE_CHUNKS:
             cols = slice(start, start + on_scalar)
@@ -104,82 +116,82 @@ def tile_picked_route2_linnone_e_kernel(tc, xT, gate, w1_words, w1_scales, offs,
                 nc.vector.tensor_copy(plane_bf16[3][:, cols], plane[3][:, cols])
                 start = cols.stop
 
-        def fetch_piece(i):
-            plain = tile(f"plain3_{i}", [P, PIECE], BF16, tag=f"plain3_{i % 2}")
-            nc.vector.tensor_copy(plain[:], looked_up(plane[3], i * PIECE, (i + 1) * PIECE))
-            return plain
+        def operand(part, tag=None):
+            codes = tile(f"codes{part.start}", [P, width(part)], U32, tag)
+            scales = tile(f"scales{part.start}", [P, width(part)], U8)
+            return codes, scales
 
-        def weave_piece(i, plain):
-            nc.vector.tensor_copy(picked[:, i * PIECE : (i + 1) * PIECE, 3], plain[:])
+        def quantise(part, codes, scales):
+            nc.vector.quantize_mx(
+                out=codes.bitcast(FP8X4), scales=scales, in_=picked[:, part, :].rearrange("p n j -> p (n j)")
+            )
 
-        def operand(start, stop):
-            if stop <= LEAD:
-                return lead_codes[:, start:stop].bitcast(FP8X4), lead_scales[:, start:stop]
-            if start >= LATE:
-                return late_codes[0][:].bitcast(FP8X4), late_scales[:]
-            return rest_codes[:, start - LEAD : stop - LEAD].bitcast(FP8X4), rest_scales[:, start - LEAD : stop - LEAD]
+        def bank(b, part):
+            return psum.tile([P, width(part)], F32, name=f"acc{part.start}_{b}")
 
-        def quantise(start, stop):
-            codes, scales = operand(start, stop)
-            nc.vector.quantize_mx(out=codes, scales=scales, in_=picked[:, start:stop, :].rearrange("p n j -> p (n j)"))
-
-        def bank(b, start, stop):
-            return psum.tile([P, stop - start], F32, name=f"acc{start}_{b}")
-
-        def product(acc, b, start, stop):
-            codes, scales = operand(start, stop)
+        def product(acc, b, codes, scales):
             nc.tensor.matmul_mx(
                 out=acc,
                 lhsT=w_codes[:, 2 * P * b : 2 * P * (b + 1)].bitcast(FP4X4),
                 lhsT_scale=w_scales[:, P * b : P * (b + 1)],
-                rhs=codes,
+                rhs=codes.bitcast(FP8X4),
                 rhs_scale=scales,
                 start=True,
                 stop=True,
             )
 
-        def scatter(b, start, stop, values):
-            nc.vector.tensor_tensor(window[b][:].indirect(entries(place, start, stop)), values, gate_sb[:, start:stop], MULT)
+        def scatter(b, part, values):
+            nc.vector.tensor_tensor(window[b][:].indirect(entries(place, part)), values, gate_sb[:, part], MULT)
 
-        nc.scalar.activation(picked[:, ON_VECTOR:LATE, 3], looked_up(plane_bf16[3], ON_VECTOR, LATE), COPY)
-        first, second = fetch_piece(0), fetch_piece(1)
-        weave_piece(0, first)
-        weave_piece(1, second)
-        lead_y = [tile("lead_y0", [P, LEAD], F32, tag="after_first_scatter"), tile("lead_y1", [P, LEAD], F32)]
-        for start in (0, PIECE):
-            quantise(start, start + PIECE)
-            acc = bank(0, start, start + PIECE)
-            product(acc[:], 0, start, start + PIECE)
-            nc.scalar.activation(lead_y[0][:, start : start + PIECE], acc[:], COPY)
-        acc = bank(1, 0, LEAD)
-        product(acc[:], 1, 0, LEAD)
+        stepped_on_scalar(3, WIDE)
+        pieces = [slice(start, start + PIECE) for start in (0, PIECE)]
+        plains = [fetch_on_vector(3, pieces[0], "first_then_fill"), fetch_on_vector(3, pieces[1])]
+        for piece, plain in zip(pieces, plains):
+            weave_on_vector(3, piece, plain)
+        fill_plain = fetch_on_vector(3, FILL, "first_then_fill")
+
+        lead_codes, lead_scales = operand(LEAD, "lead_then_late")
+        lead_y = [tile("lead_y0", [P, width(LEAD)], F32, "after_first_scatter"), tile("lead_y1", [P, width(LEAD)], F32)]
+        for piece in pieces:
+            quantise(piece, lead_codes[:, piece], lead_scales[:, piece])
+            acc = bank(0, piece)
+            product(acc[:], 0, lead_codes[:, piece], lead_scales[:, piece])
+            nc.scalar.activation(lead_y[0][:, piece], acc[:], COPY)
+        acc = bank(1, LEAD)
+        product(acc[:], 1, lead_codes[:], lead_scales[:])
         nc.scalar.activation(lead_y[1][:], acc[:], COPY)
-        quantise(ON_VECTOR, LATE)
 
-        late_plain = tile("late_plain", [P, S - LATE], BF16, tag="relay")
-        nc.scalar.activation(late_plain[:], looked_up(plane_bf16[3], LATE, S), COPY)
-        nc.scalar.activation(picked[:, LATE:S, 3], late_plain[:], COPY)
+        weave_on_vector(3, FILL, fill_plain)
+        fill_codes, fill_scales = operand(FILL)
+        quantise(FILL, fill_codes[:], fill_scales[:])
+        wide_codes, wide_scales = operand(WIDE, "first_then_fill")
+        quantise(WIDE, wide_codes[:], wide_scales[:])
 
-        rest_y = [tile(f"rest_y{b}", [P, S - LEAD], F32) for b in range(2)]
-        mid = LEAD + WIDE
+        fetch_and_weave_on_scalar(3, LATE, "lead_then_late")
+
+        rest_y = [tile(f"rest_y{b}", [P, S - LEAD.stop], F32) for b in range(2)]
+
+        def rest(b, part):
+            return rest_y[b][:, part.start - LEAD.stop : part.stop - LEAD.stop]
+
         for b in range(2):
-            acc = bank(b, LEAD, mid)
-            product(acc[:], b, LEAD, mid)
-            nc.scalar.activation(rest_y[b][:, 0:WIDE], acc[:], COPY)
+            acc = bank(b, WIDE)
+            product(acc[:], b, wide_codes[:], wide_scales[:])
+            nc.scalar.activation(rest(b, WIDE), acc[:], COPY)
 
         for b in range(2):
-            scatter(b, 0, LEAD, lead_y[b][:])
-        late_codes.append(tile("late_codes", [P, S - LATE], U32, tag="after_first_scatter"))
-        quantise(LATE, S)
+            scatter(b, LEAD, lead_y[b][:])
+        late_codes, late_scales = operand(LATE, "after_first_scatter")
+        quantise(LATE, late_codes[:], late_scales[:])
         for b in range(2):
-            acc = bank(b, mid, S)
-            product(acc[:, LATE - mid :], b, LATE, S)
-            nc.scalar.activation(rest_y[b][:, WIDE:], acc[:], COPY)
+            acc = bank(b, TAIL)
+            product(acc[:, 0 : width(FILL)], b, fill_codes[:], fill_scales[:])
+            product(acc[:, width(FILL) :], b, late_codes[:], late_scales[:])
+            nc.scalar.activation(rest(b, TAIL), acc[:], COPY)
 
-        scatter(0, LEAD, mid, rest_y[0][:, 0:WIDE])
-        scatter(1, LEAD, 2 * LEAD, rest_y[1][:, 0:LEAD])
-        scatter(0, mid, S, rest_y[0][:, WIDE:])
+        half = S // 2
+        for b, part in ((0, WIDE), (1, slice(LEAD.stop, half)), (0, TAIL), (1, slice(half, S))):
+            scatter(b, part, rest(b, part))
         for start in range(0, U, U // 4):
             nc.sync.dma_start(out=out[0:P, start : start + U // 4], in_=window[0][:, start : start + U // 4])
-        scatter(1, 2 * LEAD, S, rest_y[1][:, LEAD:])
         nc.sync.dma_start(out=out[P : 2 * P, :], in_=window[1][:])

@@ -26,7 +26,7 @@ WIDE = slice(LEAD.stop, LEAD.stop + 512)
 FILL = slice(WIDE.stop, WIDE.stop + PIECE)
 LATE = slice(FILL.stop, S)
 TAIL = slice(FILL.start, S)
-LAST_PLANE_CHUNKS = ((1344, 448), (512, 1024), (160, 416), (192, 0))
+LAST_PLANE_CHUNKS = ((1664, 0), (544, 1120), (160, 416), (192, 0))
 
 
 def width(part):

@@ -26,7 +26,7 @@ WIDE = slice(LEAD.stop, LEAD.stop + 512)
 FILL = slice(WIDE.stop, WIDE.stop + PIECE)
 LATE = slice(FILL.stop, S)
 TAIL = slice(FILL.start, S)
-LAST_PLANE_CHUNKS = ((1664, 0), (544, 1120), (160, 416), (192, 0))
+LAST_PLANE_CHUNKS = ((1536, 128), (544, 1120), (160, 416), (192, 0))
 
 
 def width(part):

@@ -22,11 +22,10 @@ STRIPE = 16
 ALIGN = 256
 PIECE = 128
 LEAD = slice(0, 2 * PIECE)
-WIDE = slice(LEAD.stop, LEAD.stop + 512)
-FILL = slice(WIDE.stop, WIDE.stop + PIECE)
-LATE = slice(FILL.stop, S)
-TAIL = slice(FILL.start, S)
-LAST_PLANE_CHUNKS = ((1536, 128), (544, 1120), (160, 416), (192, 0))
+NEXT = slice(LEAD.stop, S // 2)
+EARLY = slice(0, S // 2)
+WIDE = slice(S // 2, S)
+LAST_PLANE_CHUNKS = ((1408, 832), (448, 960), (448, 0))
 
 
 def width(part):
@@ -72,38 +71,22 @@ def tile_picked_route2_linnone_e_kernel(tc, xT, gate, w1_words, w1_scales, offs,
             cols = slice(start, start + on_scalar + on_vector)
             nc.sync.dma_start(out=plane[3][:, cols], in_=x_planes[:, 3, cols])
             start = cols.stop
-        for b in range(2):
-            cols = slice(2 * P * b, 2 * P * (b + 1))
-            nc.sync.dma_start(out=w_codes[:, cols].bitcast(I32), in_=w1_words[0][:, cols].bitcast(I32))
+        nc.sync.dma_start(out=w_codes[:].bitcast(I32), in_=w1_words[0].bitcast(I32))
         nc.sync.dma_start(place[:], dst)
-        for start in range(0, S, width(LEAD)):
-            cols = slice(start, start + width(LEAD))
-            nc.sync.dma_start(out=gate_sb[:, cols], in_=gate[:, cols])
+        nc.sync.dma_start(out=gate_sb[:], in_=gate)
 
         for b in range(2):
             nc.vector.memset(window[b][:], 0.0)
 
-        def fetch_on_vector(j, part, tag=None):
-            plain = tile(f"plain{j}_{part.start}", [P, width(part)], BF16, tag)
-            nc.vector.tensor_copy(plain[:], plane[j][:].indirect(entries(pick, part)))
-            return plain
-
-        def weave_on_vector(j, part, plain):
-            nc.vector.tensor_copy(picked[:, part, j], plain[:])
+        def stepped_on_vector(j, part):
+            nc.vector.tensor_copy(picked[:, part, j], plane[j][:].indirect(entries(pick, part)))
 
         def stepped_on_scalar(j, part):
             nc.scalar.activation(picked[:, part, j], plane_bf16[j][:].indirect(entries(pick, part)), COPY)
 
-        def fetch_and_weave_on_scalar(j, part, tag=None):
-            plain = tile(f"plain{j}_{part.start}", [P, width(part)], BF16, tag)
-            nc.scalar.activation(plain[:], plane_bf16[j][:].indirect(entries(pick, part)), COPY)
-            nc.scalar.activation(picked[:, part, j], plain[:], COPY)
-
-        for part in (LEAD, FILL):
-            weave_on_vector(2, part, fetch_on_vector(2, part))
+        stepped_on_vector(2, EARLY)
         nc.scalar.activation(plane_bf16[2][:], plane[2][:], COPY)
         stepped_on_scalar(2, WIDE)
-        fetch_and_weave_on_scalar(2, LATE)
         for j in (0, 1):
             nc.vector.tensor_copy(picked[:, :, j], plane[j][:].indirect(pick[:]))
         start = 0
@@ -144,54 +127,32 @@ def tile_picked_route2_linnone_e_kernel(tc, xT, gate, w1_words, w1_scales, offs,
             nc.vector.tensor_tensor(window[b][:].indirect(entries(place, part)), values, gate_sb[:, part], MULT)
 
         stepped_on_scalar(3, WIDE)
-        pieces = [slice(start, start + PIECE) for start in (0, PIECE)]
-        plains = [fetch_on_vector(3, pieces[0], "first_then_fill"), fetch_on_vector(3, pieces[1])]
-        for piece, plain in zip(pieces, plains):
-            weave_on_vector(3, piece, plain)
-        fill_plain = fetch_on_vector(3, FILL, "first_then_fill")
+        stepped_on_vector(3, EARLY)
 
-        lead_codes, lead_scales = operand(LEAD, "lead_then_late")
-        lead_y = [tile("lead_y0", [P, width(LEAD)], F32, "after_first_scatter"), tile("lead_y1", [P, width(LEAD)], F32)]
-        for piece in pieces:
-            quantise(piece, lead_codes[:, piece], lead_scales[:, piece])
-            acc = bank(0, piece)
-            product(acc[:], 0, lead_codes[:, piece], lead_scales[:, piece])
-            nc.scalar.activation(lead_y[0][:, piece], acc[:], COPY)
-        acc = bank(1, LEAD)
-        product(acc[:], 1, lead_codes[:], lead_scales[:])
-        nc.scalar.activation(lead_y[1][:], acc[:], COPY)
+        codes, scales = operand(slice(0, S))
+        lead_y = tile("lead_y", [P, width(LEAD)], F32)
+        rest_y = tile("rest_y", [P, S - LEAD.stop], F32)
+        other_y = tile("other_y", [P, S], F32)
 
-        weave_on_vector(3, FILL, fill_plain)
-        fill_codes, fill_scales = operand(FILL)
-        quantise(FILL, fill_codes[:], fill_scales[:])
-        wide_codes, wide_scales = operand(WIDE, "first_then_fill")
-        quantise(WIDE, wide_codes[:], wide_scales[:])
+        def multiply(b, part, values):
+            acc = bank(b, part)
+            product(acc[:], b, codes[:, part], scales[:, part])
+            nc.scalar.activation(values, acc[:], COPY)
 
-        fetch_and_weave_on_scalar(3, LATE, "lead_then_late")
+        for start in (0, PIECE):
+            piece = slice(start, start + PIECE)
+            quantise(piece, codes[:, piece], scales[:, piece])
+            multiply(0, piece, lead_y[:, piece])
+        quantise(NEXT, codes[:, NEXT], scales[:, NEXT])
+        multiply(1, EARLY, other_y[:, EARLY])
+        multiply(0, NEXT, rest_y[:, 0 : width(NEXT)])
+        quantise(WIDE, codes[:, WIDE], scales[:, WIDE])
+        multiply(0, WIDE, rest_y[:, width(NEXT) :])
+        multiply(1, WIDE, other_y[:, WIDE])
 
-        rest_y = [tile(f"rest_y{b}", [P, S - LEAD.stop], F32) for b in range(2)]
-
-        def rest(b, part):
-            return rest_y[b][:, part.start - LEAD.stop : part.stop - LEAD.stop]
-
+        scatter(0, LEAD, lead_y[:])
+        scatter(1, EARLY, other_y[:, EARLY])
+        scatter(0, slice(LEAD.stop, S), rest_y[:])
+        scatter(1, WIDE, other_y[:, WIDE])
         for b in range(2):
-            acc = bank(b, WIDE)
-            product(acc[:], b, wide_codes[:], wide_scales[:])
-            nc.scalar.activation(rest(b, WIDE), acc[:], COPY)
-
-        for b in range(2):
-            scatter(b, LEAD, lead_y[b][:])
-        late_codes, late_scales = operand(LATE, "after_first_scatter")
-        quantise(LATE, late_codes[:], late_scales[:])
-        for b in range(2):
-            acc = bank(b, TAIL)
-            product(acc[:, 0 : width(FILL)], b, fill_codes[:], fill_scales[:])
-            product(acc[:, width(FILL) :], b, late_codes[:], late_scales[:])
-            nc.scalar.activation(rest(b, TAIL), acc[:], COPY)
-
-        half = S // 2
-        for b, part in ((0, WIDE), (1, slice(LEAD.stop, half)), (0, TAIL), (1, slice(half, S))):
-            scatter(b, part, rest(b, part))
-        for start in range(0, U, U // 4):
-            nc.sync.dma_start(out=out[0:P, start : start + U // 4], in_=window[0][:, start : start + U // 4])
-        nc.sync.dma_start(out=out[P : 2 * P, :], in_=window[1][:])
+            nc.sync.dma_start(out=out[P * b : P * (b + 1), :], in_=window[b][:])

@@ -21,11 +21,9 @@ PACK = 4
 STRIPE = 16
 ALIGN = 256
 PIECE = 128
-LEAD = slice(0, 2 * PIECE)
-NEXT = slice(LEAD.stop, S // 2)
-EARLY = slice(0, S // 2)
-WIDE = slice(S // 2, S)
-LAST_PLANE_CHUNKS = ((1408, 832), (448, 960), (448, 0))
+QUARTER = S // 4
+FIRST, SECOND = slice(0, PIECE), slice(PIECE, QUARTER)
+QUARTERS = [slice(q * QUARTER, (q + 1) * QUARTER) for q in range(4)]
 
 
 def width(part):
@@ -46,17 +44,19 @@ def tile_picked_route2_linnone_e_kernel(tc, xT, gate, w1_words, w1_scales, offs,
         pick = tile("pick", [P, S // STRIPE], U16)
         place = tile("place", [P, S // STRIPE], U16)
         plane = [tile(f"plane{j}", [P, T], F32) for j in range(PACK)]
-        plane_bf16 = {j: tile(f"plane_bf16_{j}", [P, T], BF16) for j in (2, 3)}
         picked = tile("picked", [P, S, PACK], BF16)
+        codes = tile("codes", [P, S], U32)
+        scales = tile("scales", [P, S], U8)
         w_codes = tile("w_codes", [P, 2 * N], U8)
         w_scales = tile("w_scales", [P, N], U8)
         gate_sb = tile("gate_sb", [P, S], F32)
+        y = [tile(f"y{b}", [P, S], F32) for b in range(2)]
         window = [tile(f"window{b}", [P, U], F32) for b in range(2)]
 
         def entries(list_tile, part):
             return list_tile[:, part.start // STRIPE : part.stop // STRIPE]
 
-        nc.sync.dma_start(out=plane[2][:], in_=x_planes[:, 2, :])
+        nc.sync.dma_start(out=plane[0][:], in_=x_planes[:, 0, :])
         nc.sync.dma_start(pick[:], offs)
         nc.vector.memset(w_scales[:].bitcast(I32), 0)
         for q in range(4):
@@ -64,95 +64,98 @@ def tile_picked_route2_linnone_e_kernel(tc, xT, gate, w1_words, w1_scales, offs,
                 out=w_scales[32 * q : 32 * q + 4, :].bitcast(I32),
                 in_=w1_scales[0, 4 * q : 4 * q + 4, :].bitcast(I32),
             )
-        nc.sync.dma_start(out=plane[0][:], in_=x_planes[:, 0, :])
-        nc.sync.dma_start(out=plane[1][:], in_=x_planes[:, 1, :])
-        start = 0
-        for on_scalar, on_vector in LAST_PLANE_CHUNKS:
-            cols = slice(start, start + on_scalar + on_vector)
-            nc.sync.dma_start(out=plane[3][:, cols], in_=x_planes[:, 3, cols])
-            start = cols.stop
-        nc.sync.dma_start(out=w_codes[:].bitcast(I32), in_=w1_words[0].bitcast(I32))
+        for j in range(1, PACK):
+            nc.sync.dma_start(out=plane[j][:], in_=x_planes[:, j, :])
+        for b in range(2):
+            cols = slice(2 * P * b, 2 * P * (b + 1))
+            nc.sync.dma_start(out=w_codes[:, cols].bitcast(I32), in_=w1_words[0][:, cols].bitcast(I32))
+        nc.sync.dma_start(out=gate_sb[:, 0:QUARTER], in_=gate[:, 0:QUARTER])
         nc.sync.dma_start(place[:], dst)
-        nc.sync.dma_start(out=gate_sb[:], in_=gate)
+        nc.sync.dma_start(out=gate_sb[:, QUARTER:S], in_=gate[:, QUARTER:S])
 
         for b in range(2):
             nc.vector.memset(window[b][:], 0.0)
 
-        def stepped_on_vector(j, part):
-            nc.vector.tensor_copy(picked[:, part, j], plane[j][:].indirect(entries(pick, part)))
-
-        def stepped_on_scalar(j, part):
-            nc.scalar.activation(picked[:, part, j], plane_bf16[j][:].indirect(entries(pick, part)), COPY)
-
-        stepped_on_vector(2, EARLY)
-        nc.scalar.activation(plane_bf16[2][:], plane[2][:], COPY)
-        stepped_on_scalar(2, WIDE)
-        for j in (0, 1):
+        for j in range(PACK - 1):
             nc.vector.tensor_copy(picked[:, :, j], plane[j][:].indirect(pick[:]))
-        start = 0
-        for on_scalar, on_vector in LAST_PLANE_CHUNKS:
-            cols = slice(start, start + on_scalar)
-            nc.scalar.activation(plane_bf16[3][:, cols], plane[3][:, cols], COPY)
-            start = cols.stop
-            if on_vector:
-                cols = slice(start, start + on_vector)
-                nc.vector.tensor_copy(plane_bf16[3][:, cols], plane[3][:, cols])
-                start = cols.stop
 
-        def operand(part, tag=None):
-            codes = tile(f"codes{part.start}", [P, width(part)], U32, tag)
-            scales = tile(f"scales{part.start}", [P, width(part)], U8)
-            return codes, scales
+        last = PACK - 1
+        plain = {}
+        for part in (FIRST, SECOND, *QUARTERS[1:]):
+            plain[part.start] = tile(f"plain{part.start}", [P, width(part)], BF16)
+            source = plane[last][:].indirect(entries(pick, part))
+            if part is FIRST:
+                nc.vector.tensor_copy(plain[part.start][:], source)
+            else:
+                nc.scalar.activation(plain[part.start][:], source, COPY)
 
-        def quantise(part, codes, scales):
+        def weave(part):
+            nc.vector.tensor_copy(picked[:, part, last], plain[part.start][:])
+
+        def quantise(part):
             nc.vector.quantize_mx(
-                out=codes.bitcast(FP8X4), scales=scales, in_=picked[:, part, :].rearrange("p n j -> p (n j)")
+                out=codes[:, part].bitcast(FP8X4),
+                scales=scales[:, part],
+                in_=picked[:, part, :].rearrange("p n j -> p (n j)"),
             )
 
-        def bank(b, part):
-            return psum.tile([P, width(part)], F32, name=f"acc{part.start}_{b}")
-
-        def product(acc, b, codes, scales):
+        def product(b, part, tag):
+            acc = psum.tile([P, width(part)], F32, name=f"acc{part.start}_{b}", tag=tag)
             nc.tensor.matmul_mx(
-                out=acc,
+                out=acc[:],
                 lhsT=w_codes[:, 2 * P * b : 2 * P * (b + 1)].bitcast(FP4X4),
                 lhsT_scale=w_scales[:, P * b : P * (b + 1)],
-                rhs=codes.bitcast(FP8X4),
-                rhs_scale=scales,
+                rhs=codes[:, part].bitcast(FP8X4),
+                rhs_scale=scales[:, part],
                 start=True,
                 stop=True,
             )
+            return acc
 
-        def scatter(b, part, values):
-            nc.vector.tensor_tensor(window[b][:].indirect(entries(place, part)), values, gate_sb[:, part], MULT)
+        def gated_on_vector(part, acc):
+            nc.vector.tensor_tensor(y[0][:, part], acc[:], gate_sb[:, part], MULT)
 
-        stepped_on_scalar(3, WIDE)
-        stepped_on_vector(3, EARLY)
+        def plain_on_scalar(part, acc):
+            nc.scalar.activation(y[1][:, part], acc[:], COPY)
 
-        codes, scales = operand(slice(0, S))
-        lead_y = tile("lead_y", [P, width(LEAD)], F32)
-        rest_y = tile("rest_y", [P, S - LEAD.stop], F32)
-        other_y = tile("other_y", [P, S], F32)
+        def scatter_on_scalar(part):
+            nc.scalar.activation(window[0][:].indirect(entries(place, part)), y[0][:, part], COPY)
 
-        def multiply(b, part, values):
-            acc = bank(b, part)
-            product(acc[:], b, codes[:, part], scales[:, part])
-            nc.scalar.activation(values, acc[:], COPY)
+        def scatter_on_vector(part):
+            nc.vector.tensor_tensor(window[1][:].indirect(entries(place, part)), y[1][:, part], gate_sb[:, part], MULT)
 
-        for start in (0, PIECE):
-            piece = slice(start, start + PIECE)
-            quantise(piece, codes[:, piece], scales[:, piece])
-            multiply(0, piece, lead_y[:, piece])
-        quantise(NEXT, codes[:, NEXT], scales[:, NEXT])
-        multiply(1, EARLY, other_y[:, EARLY])
-        multiply(0, NEXT, rest_y[:, 0 : width(NEXT)])
-        quantise(WIDE, codes[:, WIDE], scales[:, WIDE])
-        multiply(0, WIDE, rest_y[:, width(NEXT) :])
-        multiply(1, WIDE, other_y[:, WIDE])
+        q0, q1, q2, q3 = QUARTERS
+        weave(FIRST)
+        weave(SECOND)
+        quantise(FIRST)
+        quantise(SECOND)
+        acc_first, acc_second = product(0, FIRST, "bank0"), product(0, SECOND, "bank1")
+        acc_other = product(1, q0, "bank2")
+        weave(q1)
+        gated_on_vector(FIRST, acc_first)
+        gated_on_vector(SECOND, acc_second)
+        plain_on_scalar(q0, acc_other)
+        scatter_on_scalar(q0)
 
-        scatter(0, LEAD, lead_y[:])
-        scatter(1, EARLY, other_y[:, EARLY])
-        scatter(0, slice(LEAD.stop, S), rest_y[:])
-        scatter(1, WIDE, other_y[:, WIDE])
+        quantise(q1)
+        acc1 = [product(b, q1, f"bank{3 + b}") for b in range(2)]
+        weave(q2)
+        weave(q3)
+        quantise(q2)
+        acc2 = [product(b, q2, f"bank{5 + b}") for b in range(2)]
+        gated_on_vector(q1, acc1[0])
+        plain_on_scalar(q1, acc1[1])
+        scatter_on_scalar(q1)
+        quantise(q3)
+        acc3 = [product(0, q3, "bank7"), product(1, q3, "bank0")]
+        gated_on_vector(q2, acc2[0])
+        plain_on_scalar(q2, acc2[1])
+        scatter_on_scalar(q2)
+        scatter_on_vector(q0)
+        gated_on_vector(q3, acc3[0])
+        scatter_on_scalar(q3)
+        plain_on_scalar(q3, acc3[1])
+        scatter_on_vector(slice(q1.start, q2.stop))
+        scatter_on_vector(q3)
         for b in range(2):
             nc.sync.dma_start(out=out[P * b : P * (b + 1), :], in_=window[b][:])

@@ -21,9 +21,13 @@ PACK = 4
 STRIPE = 16
 ALIGN = 256
 PIECE = 128
-QUARTER = S // 4
-FIRST, SECOND = slice(0, PIECE), slice(PIECE, QUARTER)
-QUARTERS = [slice(q * QUARTER, (q + 1) * QUARTER) for q in range(4)]
+SQUARE = 32
+FIRST, SECOND = slice(0, PIECE), slice(PIECE, 2 * PIECE)
+LEAD = slice(0, 2 * PIECE)
+MID = slice(LEAD.stop, LEAD.stop + 3 * PIECE)
+END = slice(MID.stop, S)
+MID_WIDE, MID_SHORT = slice(MID.start, S // 2), slice(S // 2, MID.stop)
+END_WIDE, END_SHORT = slice(END.start, S - PIECE), slice(S - PIECE, S)
 
 
 def width(part):
@@ -44,8 +48,8 @@ def tile_picked_route2_linnone_e_kernel(tc, xT, gate, w1_words, w1_scales, offs,
         pick = tile("pick", [P, S // STRIPE], U16)
         place = tile("place", [P, S // STRIPE], U16)
         plane = [tile(f"plane{j}", [P, T], F32) for j in range(PACK)]
-        picked = tile("picked", [P, S, PACK], BF16)
-        codes = tile("codes", [P, S], U32)
+        woven = tile("woven", [P, S * PACK], BF16)
+        picked = woven[:].rearrange("p (n j) -> p n j", j=PACK)
         scales = tile("scales", [P, S], U8)
         w_codes = tile("w_codes", [P, 2 * N], U8)
         w_scales = tile("w_scales", [P, N], U8)
@@ -58,65 +62,85 @@ def tile_picked_route2_linnone_e_kernel(tc, xT, gate, w1_words, w1_scales, offs,
 
         nc.sync.dma_start(out=plane[0][:], in_=x_planes[:, 0, :])
         nc.sync.dma_start(pick[:], offs)
+        gate_rows = tile("gate_rows", [P, SQUARE], F32)
+        nc.sync.dma_start(out=gate_rows[:], in_=gate[0 : P * SQUARE // S, :].rearrange("r (i c) -> (r i) c", c=SQUARE))
         nc.vector.memset(w_scales[:].bitcast(I32), 0)
         for q in range(4):
             nc.sync.dma_start(
                 out=w_scales[32 * q : 32 * q + 4, :].bitcast(I32),
                 in_=w1_scales[0, 4 * q : 4 * q + 4, :].bitcast(I32),
             )
-        for j in range(1, PACK):
+        nc.sync.dma_start(out=plane[1][:], in_=x_planes[:, 1, :])
+        for j in range(2, PACK):
             nc.sync.dma_start(out=plane[j][:], in_=x_planes[:, j, :])
         for b in range(2):
             cols = slice(2 * P * b, 2 * P * (b + 1))
             nc.sync.dma_start(out=w_codes[:, cols].bitcast(I32), in_=w1_words[0][:, cols].bitcast(I32))
-        nc.sync.dma_start(out=gate_sb[:, 0:QUARTER], in_=gate[:, 0:QUARTER])
         nc.sync.dma_start(place[:], dst)
-        nc.sync.dma_start(out=gate_sb[:, QUARTER:S], in_=gate[:, QUARTER:S])
 
         for b in range(2):
             nc.vector.memset(window[b][:], 0.0)
 
-        for j in range(PACK - 1):
-            nc.vector.tensor_copy(picked[:, :, j], plane[j][:].indirect(pick[:]))
+        gate_turned = tile("gate_turned", [P, SQUARE], F32)
+        nc.vector.transpose(gate_turned[:], gate_rows[:])
+        gate_spread = tile("gate_spread", [P, SQUARE, SQUARE], F32)
+        nc.scalar.activation(gate_spread[:], gate_turned[:].unsqueeze(2).to_broadcast([P, SQUARE, SQUARE]), COPY)
+        nc.vector.transpose(gate_sb[:], gate_spread[:].rearrange("p b r -> p (b r)"))
 
         last = PACK - 1
-        plain = {}
-        for part in (FIRST, SECOND, *QUARTERS[1:]):
-            plain[part.start] = tile(f"plain{part.start}", [P, width(part)], BF16)
-            source = plane[last][:].indirect(entries(pick, part))
-            if part is FIRST:
-                nc.vector.tensor_copy(plain[part.start][:], source)
-            else:
-                nc.scalar.activation(plain[part.start][:], source, COPY)
+        for j in range(last - 1):
+            nc.vector.tensor_copy(picked[:, :, j], plane[j][:].indirect(pick[:]))
+        most = slice(0, END_SHORT.start)
+        nc.vector.tensor_copy(picked[:, most, last - 1], plane[last - 1][:].indirect(entries(pick, most)))
+        pair = tile("pair", [P, 2 * PIECE], BF16)
+        nc.scalar.activation(pair[:, 0:PIECE], plane[last - 1][:].indirect(entries(pick, END_SHORT)), COPY)
+
+        plain = {part.start: tile(f"plain{part.start}", [P, width(part)], BF16)[:] for part in (FIRST, SECOND, MID_SHORT)}
+        plain[MID_WIDE.start] = tile("plain_mid", [P, width(MID_WIDE)], BF16, "mid_then_end")[:]
+        plain[END_SHORT.start] = pair[:, PIECE:]
+
+        def source(part):
+            return plane[last][:].indirect(entries(pick, part))
 
         def weave(part):
-            nc.vector.tensor_copy(picked[:, part, last], plain[part.start][:])
+            nc.vector.tensor_copy(picked[:, part, last], plain[part.start])
 
-        def quantise(part):
+        def quantise(part, codes):
             nc.vector.quantize_mx(
-                out=codes[:, part].bitcast(FP8X4),
+                out=codes.bitcast(FP8X4),
                 scales=scales[:, part],
-                in_=picked[:, part, :].rearrange("p n j -> p (n j)"),
+                in_=woven[:, PACK * part.start : PACK * part.stop],
             )
 
-        def product(b, part, tag):
-            acc = psum.tile([P, width(part)], F32, name=f"acc{part.start}_{b}", tag=tag)
+        def bank(b, part):
+            return psum.tile([P, width(part)], F32, name=f"acc{part.start}_{b}")[:]
+
+        def within(part, whole):
+            return slice(part.start - whole.start, part.stop - whole.start)
+
+        def product(b, part, acc, codes):
             nc.tensor.matmul_mx(
-                out=acc[:],
+                out=acc,
                 lhsT=w_codes[:, 2 * P * b : 2 * P * (b + 1)].bitcast(FP4X4),
                 lhsT_scale=w_scales[:, P * b : P * (b + 1)],
-                rhs=codes[:, part].bitcast(FP8X4),
+                rhs=codes.bitcast(FP8X4),
                 rhs_scale=scales[:, part],
                 start=True,
                 stop=True,
             )
+
+        def quantise_and_multiply(whole, pieces, blocks, tag=None):
+            acc = [bank(b, whole) for b in range(2)]
+            codes = tile(f"codes{whole.start}", [P, width(whole)], U32, tag)
+            for piece in pieces:
+                quantise(piece, codes[:, within(piece, whole)])
+            for b in blocks:
+                for piece in pieces:
+                    product(b, piece, acc[b][:, within(piece, whole)], codes[:, within(piece, whole)])
             return acc
 
         def gated_on_vector(part, acc):
-            nc.vector.tensor_tensor(y[0][:, part], acc[:], gate_sb[:, part], MULT)
-
-        def plain_on_scalar(part, acc):
-            nc.scalar.activation(y[1][:, part], acc[:], COPY)
+            nc.vector.tensor_tensor(y[0][:, part], acc, gate_sb[:, part], MULT)
 
         def scatter_on_scalar(part):
             nc.scalar.activation(window[0][:].indirect(entries(place, part)), y[0][:, part], COPY)
@@ -124,38 +148,40 @@ def tile_picked_route2_linnone_e_kernel(tc, xT, gate, w1_words, w1_scales, offs,
         def scatter_on_vector(part):
             nc.vector.tensor_tensor(window[1][:].indirect(entries(place, part)), y[1][:, part], gate_sb[:, part], MULT)
 
-        q0, q1, q2, q3 = QUARTERS
+        nc.vector.tensor_copy(plain[FIRST.start], source(FIRST))
+        for part in (SECOND, MID_SHORT, MID_WIDE, END_SHORT):
+            nc.scalar.activation(plain[part.start], source(part), COPY)
         weave(FIRST)
         weave(SECOND)
-        quantise(FIRST)
-        quantise(SECOND)
-        acc_first, acc_second = product(0, FIRST, "bank0"), product(0, SECOND, "bank1")
-        acc_other = product(1, q0, "bank2")
-        weave(q1)
-        gated_on_vector(FIRST, acc_first)
-        gated_on_vector(SECOND, acc_second)
-        plain_on_scalar(q0, acc_other)
-        scatter_on_scalar(q0)
+        lead_codes = tile("lead_codes", [P, width(LEAD)], U32, "lead_then_mid")
+        lead = {}
+        for piece in (FIRST, SECOND):
+            quantise(piece, lead_codes[:, piece])
+            lead[piece.start] = bank(0, piece)
+            product(0, piece, lead[piece.start], lead_codes[:, piece])
+        lead_other = bank(1, LEAD)
+        product(1, LEAD, lead_other, lead_codes[:])
+        nc.scalar.activation(picked[:, END_SHORT, last - 1 :], pair[:].rearrange("p (j n) -> p n j", j=2), COPY)
+        weave(MID_SHORT)
+        weave(MID_WIDE)
+        plain[END_WIDE.start] = tile("plain_end", [P, width(END_WIDE)], BF16, "mid_then_end")[:]
+        nc.scalar.activation(plain[END_WIDE.start], source(END_WIDE), COPY)
+        for piece in (FIRST, SECOND):
+            gated_on_vector(piece, lead[piece.start])
+        scatter_on_scalar(LEAD)
 
-        quantise(q1)
-        acc1 = [product(b, q1, f"bank{3 + b}") for b in range(2)]
-        weave(q2)
-        weave(q3)
-        quantise(q2)
-        acc2 = [product(b, q2, f"bank{5 + b}") for b in range(2)]
-        gated_on_vector(q1, acc1[0])
-        plain_on_scalar(q1, acc1[1])
-        scatter_on_scalar(q1)
-        quantise(q3)
-        acc3 = [product(0, q3, "bank7"), product(1, q3, "bank0")]
-        gated_on_vector(q2, acc2[0])
-        plain_on_scalar(q2, acc2[1])
-        scatter_on_scalar(q2)
-        scatter_on_vector(q0)
-        gated_on_vector(q3, acc3[0])
-        scatter_on_scalar(q3)
-        plain_on_scalar(q3, acc3[1])
-        scatter_on_vector(slice(q1.start, q2.stop))
-        scatter_on_vector(q3)
-        for b in range(2):
-            nc.sync.dma_start(out=out[P * b : P * (b + 1), :], in_=window[b][:])
+        mid = quantise_and_multiply(MID, (MID_WIDE, MID_SHORT), (0, 1), "lead_then_mid")
+        weave(END_WIDE)
+        nc.vector.tensor_copy(y[1][:, LEAD], lead_other)
+        gated_on_vector(MID, mid[0])
+        nc.scalar.activation(y[1][:, MID], mid[1], COPY)
+        scatter_on_scalar(MID)
+        end = quantise_and_multiply(END, (END_WIDE, END_SHORT), (1, 0))
+        scatter_on_vector(LEAD)
+        nc.vector.tensor_copy(y[1][:, END], end[1])
+        gated_on_vector(END, end[0])
+        scatter_on_scalar(END)
+        scatter_on_vector(slice(LEAD.stop, S))
+        for cols in (slice(0, U // 2), slice(U // 2, U)):
+            nc.sync.dma_start(out=out[0:P, cols], in_=window[0][:, cols])
+        nc.sync.dma_start(out=out[P : 2 * P, :], in_=window[1][:])

@@ -50,6 +50,7 @@ def tile_picked_route2_linnone_e_kernel(tc, xT, gate, w1_words, w1_scales, offs,
         plane = [tile(f"plane{j}", [P, T], F32) for j in range(PACK)]
         woven = tile("woven", [P, S * PACK], BF16)
         picked = woven[:].rearrange("p (n j) -> p n j", j=PACK)
+        codes = tile("codes", [P, S], U32)
         scales = tile("scales", [P, S], U8)
         w_codes = tile("w_codes", [P, 2 * N], U8)
         w_scales = tile("w_scales", [P, N], U8)
@@ -95,8 +96,7 @@ def tile_picked_route2_linnone_e_kernel(tc, xT, gate, w1_words, w1_scales, offs,
         pair = tile("pair", [P, 2 * PIECE], BF16)
         nc.scalar.activation(pair[:, 0:PIECE], plane[last - 1][:].indirect(entries(pick, END_SHORT)), COPY)
 
-        plain = {part.start: tile(f"plain{part.start}", [P, width(part)], BF16)[:] for part in (FIRST, SECOND, MID_SHORT)}
-        plain[MID_WIDE.start] = tile("plain_mid", [P, width(MID_WIDE)], BF16, "mid_then_end")[:]
+        plain = {part.start: tile(f"plain{part.start}", [P, width(part)], BF16)[:] for part in (LEAD, MID_SHORT, MID_WIDE, END_WIDE)}
         plain[END_SHORT.start] = pair[:, PIECE:]
 
         def source(part):
@@ -105,39 +105,27 @@ def tile_picked_route2_linnone_e_kernel(tc, xT, gate, w1_words, w1_scales, offs,
         def weave(part):
             nc.vector.tensor_copy(picked[:, part, last], plain[part.start])
 
-        def quantise(part, codes):
+        def quantise(part):
             nc.vector.quantize_mx(
-                out=codes.bitcast(FP8X4),
+                out=codes[:, part].bitcast(FP8X4),
                 scales=scales[:, part],
                 in_=woven[:, PACK * part.start : PACK * part.stop],
             )
 
-        def bank(b, part):
-            return psum.tile([P, width(part)], F32, name=f"acc{part.start}_{b}")[:]
-
-        def within(part, whole):
-            return slice(part.start - whole.start, part.stop - whole.start)
-
-        def product(b, part, acc, codes):
-            nc.tensor.matmul_mx(
-                out=acc,
-                lhsT=w_codes[:, 2 * P * b : 2 * P * (b + 1)].bitcast(FP4X4),
-                lhsT_scale=w_scales[:, P * b : P * (b + 1)],
-                rhs=codes.bitcast(FP8X4),
-                rhs_scale=scales[:, part],
-                start=True,
-                stop=True,
-            )
-
-        def quantise_and_multiply(whole, pieces, blocks, tag=None):
-            acc = [bank(b, whole) for b in range(2)]
-            codes = tile(f"codes{whole.start}", [P, width(whole)], U32, tag)
+        def multiply(b, *pieces):
+            first = pieces[0].start
+            acc = psum.tile([P, pieces[-1].stop - first], F32, name=f"acc{first}_{b}")
             for piece in pieces:
-                quantise(piece, codes[:, within(piece, whole)])
-            for b in blocks:
-                for piece in pieces:
-                    product(b, piece, acc[b][:, within(piece, whole)], codes[:, within(piece, whole)])
-            return acc
+                nc.tensor.matmul_mx(
+                    out=acc[:, piece.start - first : piece.stop - first],
+                    lhsT=w_codes[:, 2 * P * b : 2 * P * (b + 1)].bitcast(FP4X4),
+                    lhsT_scale=w_scales[:, P * b : P * (b + 1)],
+                    rhs=codes[:, piece].bitcast(FP8X4),
+                    rhs_scale=scales[:, piece],
+                    start=True,
+                    stop=True,
+                )
+            return acc[:]
 
         def gated_on_vector(part, acc):
             nc.vector.tensor_tensor(y[0][:, part], acc, gate_sb[:, part], MULT)
@@ -148,40 +136,41 @@ def tile_picked_route2_linnone_e_kernel(tc, xT, gate, w1_words, w1_scales, offs,
         def scatter_on_vector(part):
             nc.vector.tensor_tensor(window[1][:].indirect(entries(place, part)), y[1][:, part], gate_sb[:, part], MULT)
 
-        nc.vector.tensor_copy(plain[FIRST.start], source(FIRST))
-        for part in (SECOND, MID_SHORT, MID_WIDE, END_SHORT):
+        nc.vector.tensor_copy(plain[LEAD.start][:, FIRST], source(FIRST))
+        nc.scalar.activation(plain[LEAD.start][:, SECOND], source(SECOND), COPY)
+        for part in (MID_SHORT, MID_WIDE, END_SHORT, END_WIDE):
             nc.scalar.activation(plain[part.start], source(part), COPY)
-        weave(FIRST)
-        weave(SECOND)
-        lead_codes = tile("lead_codes", [P, width(LEAD)], U32, "lead_then_mid")
-        lead = {}
-        for piece in (FIRST, SECOND):
-            quantise(piece, lead_codes[:, piece])
-            lead[piece.start] = bank(0, piece)
-            product(0, piece, lead[piece.start], lead_codes[:, piece])
-        lead_other = bank(1, LEAD)
-        product(1, LEAD, lead_other, lead_codes[:])
-        nc.scalar.activation(picked[:, END_SHORT, last - 1 :], pair[:].rearrange("p (j n) -> p n j", j=2), COPY)
+        weave(LEAD)
         weave(MID_SHORT)
-        weave(MID_WIDE)
-        plain[END_WIDE.start] = tile("plain_end", [P, width(END_WIDE)], BF16, "mid_then_end")[:]
-        nc.scalar.activation(plain[END_WIDE.start], source(END_WIDE), COPY)
+        lead = []
         for piece in (FIRST, SECOND):
-            gated_on_vector(piece, lead[piece.start])
+            quantise(piece)
+            lead.append(multiply(0, piece))
+        nc.scalar.activation(picked[:, END_SHORT, last - 1 :], pair[:].rearrange("p (j n) -> p n j", j=2), COPY)
+        weave(MID_WIDE)
+        for piece, acc in zip((FIRST, SECOND), lead):
+            gated_on_vector(piece, acc)
         scatter_on_scalar(LEAD)
 
-        mid = quantise_and_multiply(MID, (MID_WIDE, MID_SHORT), (0, 1), "lead_then_mid")
+        quantise(MID_WIDE)
+        quantise(MID_SHORT)
+        mid = multiply(0, MID_WIDE, MID_SHORT)
+        third, fourth = slice(LEAD.stop, LEAD.stop + PIECE), slice(LEAD.stop + PIECE, S // 2)
+        early_other, fourth_other = multiply(1, LEAD, third), multiply(1, fourth)
         weave(END_WIDE)
-        nc.vector.tensor_copy(y[1][:, LEAD], lead_other)
-        gated_on_vector(MID, mid[0])
-        nc.scalar.activation(y[1][:, MID], mid[1], COPY)
+        quantise(END_SHORT)
+        quantise(END_WIDE)
+        end_other = multiply(1, MID_SHORT, END_WIDE, END_SHORT)
+        end = multiply(0, END_WIDE, END_SHORT)
+        gated_on_vector(MID, mid)
+        nc.scalar.activation(y[1][:, fourth], fourth_other, COPY)
         scatter_on_scalar(MID)
-        end = quantise_and_multiply(END, (END_WIDE, END_SHORT), (1, 0))
-        scatter_on_vector(LEAD)
-        nc.vector.tensor_copy(y[1][:, END], end[1])
-        gated_on_vector(END, end[0])
+
+        nc.vector.tensor_copy(y[1][:, 0 : third.stop], early_other)
+        nc.vector.tensor_copy(y[1][:, S // 2 : S], end_other)
+        gated_on_vector(END, end)
         scatter_on_scalar(END)
-        scatter_on_vector(slice(LEAD.stop, S))
+        scatter_on_vector(slice(0, S))
         for cols in (slice(0, U // 2), slice(U // 2, U)):
             nc.sync.dma_start(out=out[0:P, cols], in_=window[0][:, cols])
         nc.sync.dma_start(out=out[P : 2 * P, :], in_=window[1][:])

@@ -62,9 +62,9 @@ def tile_picked_route2_linnone_e_kernel(tc, xT, gate, w1_words, w1_scales, offs,
             return list_tile[:, part.start // STRIPE : part.stop // STRIPE]
 
         nc.sync.dma_start(out=plane[0][:], in_=x_planes[:, 0, :])
-        nc.sync.dma_start(pick[:], offs)
         gate_rows = tile("gate_rows", [P, SQUARE], F32)
-        nc.sync.dma_start(out=gate_rows[:], in_=gate[0 : P * SQUARE // S, :].rearrange("r (i c) -> (r i) c", c=SQUARE))
+        nc.scalar.dma_start(out=gate_rows[:], in_=gate[0 : P * SQUARE // S, :].rearrange("r (i c) -> (r i) c", c=SQUARE))
+        nc.sync.dma_start(pick[:], offs)
         nc.vector.memset(w_scales[:].bitcast(I32), 0)
         for q in range(4):
             nc.sync.dma_start(
@@ -156,21 +156,20 @@ def tile_picked_route2_linnone_e_kernel(tc, xT, gate, w1_words, w1_scales, offs,
         quantise(MID_SHORT)
         mid = multiply(0, MID_WIDE, MID_SHORT)
         third, fourth = slice(LEAD.stop, LEAD.stop + PIECE), slice(LEAD.stop + PIECE, S // 2)
-        early_other, fourth_other = multiply(1, LEAD, third), multiply(1, fourth)
+        early_other, fourth_other = multiply(1, LEAD, third), multiply(1, fourth, MID_SHORT)
         weave(END_WIDE)
         quantise(END_SHORT)
         quantise(END_WIDE)
-        end_other = multiply(1, MID_SHORT, END_WIDE, END_SHORT)
+        end_other = multiply(1, END_WIDE, END_SHORT)
         end = multiply(0, END_WIDE, END_SHORT)
         gated_on_vector(MID, mid)
-        nc.scalar.activation(y[1][:, fourth], fourth_other, COPY)
+        nc.scalar.activation(y[1][:, fourth.start : MID.stop], fourth_other, COPY)
         scatter_on_scalar(MID)
 
         nc.vector.tensor_copy(y[1][:, 0 : third.stop], early_other)
-        nc.vector.tensor_copy(y[1][:, S // 2 : S], end_other)
+        nc.vector.tensor_copy(y[1][:, END], end_other)
         gated_on_vector(END, end)
         scatter_on_scalar(END)
         scatter_on_vector(slice(0, S))
-        for cols in (slice(0, U // 2), slice(U // 2, U)):
-            nc.sync.dma_start(out=out[0:P, cols], in_=window[0][:, cols])
-        nc.sync.dma_start(out=out[P : 2 * P, :], in_=window[1][:])
+        for b in range(2):
+            nc.sync.dma_start(out=out[P * b : P * (b + 1), :], in_=window[b][:])

@@ -22,16 +22,22 @@ STRIPE = 16
 ALIGN = 256
 PIECE = 128
 SQUARE = 32
-FIRST, SECOND = slice(0, PIECE), slice(PIECE, 2 * PIECE)
-LEAD = slice(0, 2 * PIECE)
-MID = slice(LEAD.stop, LEAD.stop + 3 * PIECE)
-END = slice(MID.stop, S)
-MID_WIDE, MID_SHORT = slice(MID.start, S // 2), slice(S // 2, MID.stop)
-END_WIDE, END_SHORT = slice(END.start, S - PIECE), slice(S - PIECE, S)
+
+
+def pieces(first, stop):
+    return slice(first * PIECE, stop * PIECE)
+
+
+def piece(i):
+    return pieces(i, i + 1)
 
 
 def width(part):
     return part.stop - part.start
+
+
+LEAD, MID, END = pieces(0, 2), pieces(2, 5), pieces(5, 8)
+PAIRED = pieces(6, 8)
 
 
 def tile_picked_route2_linnone_e_kernel(tc, xT, gate, w1_words, w1_scales, offs, dst, out):
@@ -42,8 +48,8 @@ def tile_picked_route2_linnone_e_kernel(tc, xT, gate, w1_words, w1_scales, offs,
         keep = ctx.enter_context(tc.tile_pool(name="keep", bufs=1))
         psum = ctx.enter_context(tc.psum_pool(name="psum", bufs=1))
 
-        def tile(name, shape, dtype, tag=None):
-            return keep.tile(shape, dtype, name=name, tag=tag or name, align_bytes=ALIGN)
+        def tile(name, shape, dtype):
+            return keep.tile(shape, dtype, name=name, align_bytes=ALIGN)
 
         pick = tile("pick", [P, S // STRIPE], U16)
         place = tile("place", [P, S // STRIPE], U16)
@@ -57,6 +63,8 @@ def tile_picked_route2_linnone_e_kernel(tc, xT, gate, w1_words, w1_scales, offs,
         gate_sb = tile("gate_sb", [P, S], F32)
         y = [tile(f"y{b}", [P, S], F32) for b in range(2)]
         window = [tile(f"window{b}", [P, U], F32) for b in range(2)]
+        plain = tile("plain", [P, PAIRED.start], BF16)
+        pair = tile("pair", [P, 2, width(PAIRED)], BF16)
 
         def entries(list_tile, part):
             return list_tile[:, part.start // STRIPE : part.stop // STRIPE]
@@ -71,8 +79,7 @@ def tile_picked_route2_linnone_e_kernel(tc, xT, gate, w1_words, w1_scales, offs,
                 out=w_scales[32 * q : 32 * q + 4, :].bitcast(I32),
                 in_=w1_scales[0, 4 * q : 4 * q + 4, :].bitcast(I32),
             )
-        nc.sync.dma_start(out=plane[1][:], in_=x_planes[:, 1, :])
-        for j in range(2, PACK):
+        for j in range(1, PACK):
             nc.sync.dma_start(out=plane[j][:], in_=x_planes[:, j, :])
         for b in range(2):
             cols = slice(2 * P * b, 2 * P * (b + 1))
@@ -89,21 +96,24 @@ def tile_picked_route2_linnone_e_kernel(tc, xT, gate, w1_words, w1_scales, offs,
         nc.vector.transpose(gate_sb[:], gate_spread[:].rearrange("p b r -> p (b r)"))
 
         last = PACK - 1
+
+        def source(j, part):
+            return plane[j][:].indirect(entries(pick, part))
+
         for j in range(last - 1):
-            nc.vector.tensor_copy(picked[:, :, j], plane[j][:].indirect(pick[:]))
-        most = slice(0, END_SHORT.start)
-        nc.vector.tensor_copy(picked[:, most, last - 1], plane[last - 1][:].indirect(entries(pick, most)))
-        pair = tile("pair", [P, 2 * PIECE], BF16)
-        nc.scalar.activation(pair[:, 0:PIECE], plane[last - 1][:].indirect(entries(pick, END_SHORT)), COPY)
+            nc.vector.tensor_copy(picked[:, :, j], source(j, slice(0, S)))
+        unpaired = slice(0, PAIRED.start)
+        nc.vector.tensor_copy(picked[:, unpaired, last - 1], source(last - 1, unpaired))
+        nc.scalar.activation(pair[:, 0, :], source(last - 1, PAIRED), COPY)
 
-        plain = {part.start: tile(f"plain{part.start}", [P, width(part)], BF16)[:] for part in (LEAD, MID_SHORT, MID_WIDE, END_WIDE)}
-        plain[END_SHORT.start] = pair[:, PIECE:]
+        def fetch_on_vector(part):
+            nc.vector.tensor_copy(plain[:, part], source(last, part))
 
-        def source(part):
-            return plane[last][:].indirect(entries(pick, part))
+        def fetch_on_scalar(part):
+            nc.scalar.activation(plain[:, part], source(last, part), COPY)
 
         def weave(part):
-            nc.vector.tensor_copy(picked[:, part, last], plain[part.start])
+            nc.vector.tensor_copy(picked[:, part, last], plain[:, part])
 
         def quantise(part):
             nc.vector.quantize_mx(
@@ -112,16 +122,16 @@ def tile_picked_route2_linnone_e_kernel(tc, xT, gate, w1_words, w1_scales, offs,
                 in_=woven[:, PACK * part.start : PACK * part.stop],
             )
 
-        def multiply(b, *pieces):
-            first = pieces[0].start
-            acc = psum.tile([P, pieces[-1].stop - first], F32, name=f"acc{first}_{b}")
-            for piece in pieces:
+        def multiply(b, *parts):
+            first = parts[0].start
+            acc = psum.tile([P, parts[-1].stop - first], F32, name=f"acc{first}_{b}")
+            for part in parts:
                 nc.tensor.matmul_mx(
-                    out=acc[:, piece.start - first : piece.stop - first],
+                    out=acc[:, part.start - first : part.stop - first],
                     lhsT=w_codes[:, 2 * P * b : 2 * P * (b + 1)].bitcast(FP4X4),
                     lhsT_scale=w_scales[:, P * b : P * (b + 1)],
-                    rhs=codes[:, piece].bitcast(FP8X4),
-                    rhs_scale=scales[:, piece],
+                    rhs=codes[:, part].bitcast(FP8X4),
+                    rhs_scale=scales[:, part],
                     start=True,
                     stop=True,
                 )
@@ -136,40 +146,44 @@ def tile_picked_route2_linnone_e_kernel(tc, xT, gate, w1_words, w1_scales, offs,
         def scatter_on_vector(part):
             nc.vector.tensor_tensor(window[1][:].indirect(entries(place, part)), y[1][:, part], gate_sb[:, part], MULT)
 
-        nc.vector.tensor_copy(plain[LEAD.start][:, FIRST], source(FIRST))
-        nc.scalar.activation(plain[LEAD.start][:, SECOND], source(SECOND), COPY)
-        for part in (MID_SHORT, MID_WIDE, END_SHORT, END_WIDE):
-            nc.scalar.activation(plain[part.start], source(part), COPY)
-        weave(LEAD)
-        weave(MID_SHORT)
+        fetch_on_vector(piece(0))
+        fetch_on_vector(piece(2))
+        fetch_on_scalar(piece(1))
+        fetch_on_scalar(pieces(3, 5))
+        nc.scalar.activation(pair[:, 1, :], source(last, PAIRED), COPY)
+        fetch_on_scalar(piece(5))
+        nc.scalar.activation(picked[:, PAIRED, last - 1 :], pair[:].rearrange("p j n -> p n j"), COPY)
+
+        weave(piece(0))
+        weave(piece(1))
         lead = []
-        for piece in (FIRST, SECOND):
-            quantise(piece)
-            lead.append(multiply(0, piece))
-        nc.scalar.activation(picked[:, END_SHORT, last - 1 :], pair[:].rearrange("p (j n) -> p n j", j=2), COPY)
-        weave(MID_WIDE)
-        for piece, acc in zip((FIRST, SECOND), lead):
-            gated_on_vector(piece, acc)
+        for i in range(2):
+            quantise(piece(i))
+            lead.append(multiply(0, piece(i)))
+        lead_other = multiply(1, LEAD)
+        weave(pieces(2, 4))
+        for i in range(2):
+            gated_on_vector(piece(i), lead[i])
         scatter_on_scalar(LEAD)
 
-        quantise(MID_WIDE)
-        quantise(MID_SHORT)
-        mid = multiply(0, MID_WIDE, MID_SHORT)
-        third, fourth = slice(LEAD.stop, LEAD.stop + PIECE), slice(LEAD.stop + PIECE, S // 2)
-        early_other, fourth_other = multiply(1, LEAD, third), multiply(1, fourth, MID_SHORT)
-        weave(END_WIDE)
-        quantise(END_SHORT)
-        quantise(END_WIDE)
-        end_other = multiply(1, END_WIDE, END_SHORT)
-        end = multiply(0, END_WIDE, END_SHORT)
+        weave(piece(4))
+        quantise(pieces(2, 4))
+        quantise(piece(4))
+        mid = multiply(0, pieces(2, 4), piece(4))
+        mid_other = multiply(1, pieces(2, 4))
+        weave(piece(5))
+        nc.vector.tensor_copy(y[1][:, LEAD], lead_other)
+        quantise(END)
+        end_other = multiply(1, pieces(4, 8))
+        end = multiply(0, pieces(5, 7), piece(7))
         gated_on_vector(MID, mid)
-        nc.scalar.activation(y[1][:, fourth.start : MID.stop], fourth_other, COPY)
+        nc.scalar.activation(y[1][:, pieces(2, 4)], mid_other, COPY)
         scatter_on_scalar(MID)
 
-        nc.vector.tensor_copy(y[1][:, 0 : third.stop], early_other)
-        nc.vector.tensor_copy(y[1][:, END], end_other)
+        scatter_on_vector(LEAD)
+        nc.vector.tensor_copy(y[1][:, pieces(4, 8)], end_other)
         gated_on_vector(END, end)
         scatter_on_scalar(END)
-        scatter_on_vector(slice(0, S))
+        scatter_on_vector(slice(LEAD.stop, S))
         for b in range(2):
             nc.sync.dma_start(out=out[P * b : P * (b + 1), :], in_=window[b][:])

@@ -37,7 +37,7 @@ def width(part):
 
 
 LEAD, MID, END = pieces(0, 2), pieces(2, 5), pieces(5, 8)
-PAIRED = pieces(6, 8)
+EARLY, PAIRED, LATE = pieces(0, 4), piece(4), END
 
 
 def tile_picked_route2_linnone_e_kernel(tc, xT, gate, w1_words, w1_scales, offs, dst, out):
@@ -56,14 +56,13 @@ def tile_picked_route2_linnone_e_kernel(tc, xT, gate, w1_words, w1_scales, offs,
         plane = [tile(f"plane{j}", [P, T], F32) for j in range(PACK)]
         woven = tile("woven", [P, S * PACK], BF16)
         picked = woven[:].rearrange("p (n j) -> p n j", j=PACK)
-        codes = tile("codes", [P, S], U32)
         scales = tile("scales", [P, S], U8)
         w_codes = tile("w_codes", [P, 2 * N], U8)
         w_scales = tile("w_scales", [P, N], U8)
         gate_sb = tile("gate_sb", [P, S], F32)
         y = [tile(f"y{b}", [P, S], F32) for b in range(2)]
         window = [tile(f"window{b}", [P, U], F32) for b in range(2)]
-        plain = tile("plain", [P, PAIRED.start], BF16)
+        plain = tile("plain", [P, S], BF16)
         pair = tile("pair", [P, 2, width(PAIRED)], BF16)
 
         def entries(list_tile, part):
@@ -102,9 +101,10 @@ def tile_picked_route2_linnone_e_kernel(tc, xT, gate, w1_words, w1_scales, offs,
 
         for j in range(last - 1):
             nc.vector.tensor_copy(picked[:, :, j], source(j, slice(0, S)))
-        unpaired = slice(0, PAIRED.start)
-        nc.vector.tensor_copy(picked[:, unpaired, last - 1], source(last - 1, unpaired))
+        nc.vector.tensor_copy(picked[:, EARLY, last - 1], source(last - 1, EARLY))
+        nc.scalar.activation(plain[:, LATE], source(last - 1, LATE), COPY)
         nc.scalar.activation(pair[:, 0, :], source(last - 1, PAIRED), COPY)
+        nc.vector.tensor_copy(picked[:, LATE, last - 1], plain[:, LATE])
 
         def fetch_on_vector(part):
             nc.vector.tensor_copy(plain[:, part], source(last, part))
@@ -115,9 +115,20 @@ def tile_picked_route2_linnone_e_kernel(tc, xT, gate, w1_words, w1_scales, offs,
         def weave(part):
             nc.vector.tensor_copy(picked[:, part, last], plain[:, part])
 
+        codes = {}
+
+        def new_codes(part, tag):
+            made = keep.tile([P, width(part)], U32, name=f"codes{part.start}", tag=tag, align_bytes=ALIGN)
+            for i in range(part.start // PIECE, part.stop // PIECE):
+                codes[i] = (made, part.start)
+
+        def codes_of(part):
+            made, first = codes[part.start // PIECE]
+            return made[:, part.start - first : part.stop - first].bitcast(FP8X4)
+
         def quantise(part):
             nc.vector.quantize_mx(
-                out=codes[:, part].bitcast(FP8X4),
+                out=codes_of(part),
                 scales=scales[:, part],
                 in_=woven[:, PACK * part.start : PACK * part.stop],
             )
@@ -130,7 +141,7 @@ def tile_picked_route2_linnone_e_kernel(tc, xT, gate, w1_words, w1_scales, offs,
                     out=acc[:, part.start - first : part.stop - first],
                     lhsT=w_codes[:, 2 * P * b : 2 * P * (b + 1)].bitcast(FP4X4),
                     lhsT_scale=w_scales[:, P * b : P * (b + 1)],
-                    rhs=codes[:, part].bitcast(FP8X4),
+                    rhs=codes_of(part),
                     rhs_scale=scales[:, part],
                     start=True,
                     stop=True,
@@ -149,11 +160,13 @@ def tile_picked_route2_linnone_e_kernel(tc, xT, gate, w1_words, w1_scales, offs,
         fetch_on_vector(piece(0))
         fetch_on_vector(piece(2))
         fetch_on_scalar(piece(1))
-        fetch_on_scalar(pieces(3, 5))
         nc.scalar.activation(pair[:, 1, :], source(last, PAIRED), COPY)
+        fetch_on_scalar(piece(3))
         fetch_on_scalar(piece(5))
         nc.scalar.activation(picked[:, PAIRED, last - 1 :], pair[:].rearrange("p j n -> p n j"), COPY)
+        fetch_on_scalar(pieces(6, 8))
 
+        new_codes(LEAD, "lead_codes")
         weave(piece(0))
         weave(piece(1))
         lead = []
@@ -166,22 +179,22 @@ def tile_picked_route2_linnone_e_kernel(tc, xT, gate, w1_words, w1_scales, offs,
             gated_on_vector(piece(i), lead[i])
         scatter_on_scalar(LEAD)
 
-        weave(piece(4))
-        quantise(pieces(2, 4))
-        quantise(piece(4))
+        new_codes(MID, "later_codes")
+        quantise(MID)
         mid = multiply(0, pieces(2, 4), piece(4))
-        mid_other = multiply(1, pieces(2, 4))
-        weave(piece(5))
+        mid_other = multiply(1, pieces(2, 4), piece(4))
+        weave(LATE)
         nc.vector.tensor_copy(y[1][:, LEAD], lead_other)
-        quantise(END)
-        end_other = multiply(1, pieces(4, 8))
-        end = multiply(0, pieces(5, 7), piece(7))
         gated_on_vector(MID, mid)
-        nc.scalar.activation(y[1][:, pieces(2, 4)], mid_other, COPY)
+        nc.scalar.activation(y[1][:, MID], mid_other, COPY)
         scatter_on_scalar(MID)
+        new_codes(END, "later_codes")
+        quantise(END)
+        end_other = multiply(1, pieces(5, 7), piece(7))
+        end = multiply(0, pieces(5, 7), piece(7))
 
         scatter_on_vector(LEAD)
-        nc.vector.tensor_copy(y[1][:, pieces(4, 8)], end_other)
+        nc.vector.tensor_copy(y[1][:, END], end_other)
         gated_on_vector(END, end)
         scatter_on_scalar(END)
         scatter_on_vector(slice(LEAD.stop, S))

@@ -15,6 +15,7 @@ FP8X4 = mybir.dt.float8_e4m3fn_x4
 FP4X4 = mybir.dt.float4_e2m1fn_x4
 COPY = mybir.ActivationFunctionType.Copy
 MULT = mybir.AluOpType.mult
+ADD = mybir.AluOpType.add
 
 P = 128
 PACK = 4
@@ -37,6 +38,7 @@ def width(part):
 
 
 LEAD, MID, END = pieces(0, 2), pieces(2, 5), pieces(5, 8)
+FILL = slice(0, 3 * PIECE // 2)
 EARLY, PAIRED, LATE = pieces(0, 4), piece(4), END
 
 
@@ -78,15 +80,18 @@ def tile_picked_route2_linnone_e_kernel(tc, xT, gate, w1_words, w1_scales, offs,
                 out=w_scales[32 * q : 32 * q + 4, :].bitcast(I32),
                 in_=w1_scales[0, 4 * q : 4 * q + 4, :].bitcast(I32),
             )
-        for j in range(1, PACK):
+        nc.sync.dma_start(out=plane[1][:], in_=x_planes[:, 1, :])
+        nc.sync.dma_start(place[:], dst)
+        for j in range(2, PACK):
             nc.sync.dma_start(out=plane[j][:], in_=x_planes[:, j, :])
         for b in range(2):
             cols = slice(2 * P * b, 2 * P * (b + 1))
             nc.sync.dma_start(out=w_codes[:, cols].bitcast(I32), in_=w1_words[0][:, cols].bitcast(I32))
-        nc.sync.dma_start(place[:], dst)
 
         for b in range(2):
             nc.vector.memset(window[b][:], 0.0)
+        zeros = tile("zeros", [P, width(FILL)], F32)
+        nc.vector.memset(zeros[:], 0.0)
 
         gate_turned = tile("gate_turned", [P, SQUARE], F32)
         nc.vector.transpose(gate_turned[:], gate_rows[:])
@@ -184,7 +189,8 @@ def tile_picked_route2_linnone_e_kernel(tc, xT, gate, w1_words, w1_scales, offs,
         mid = multiply(0, pieces(2, 4), piece(4))
         mid_other = multiply(1, pieces(2, 4), piece(4))
         weave(LATE)
-        nc.vector.tensor_copy(y[1][:, LEAD], lead_other)
+        nc.vector.tensor_tensor(y[1][:, FILL], lead_other[:, FILL], gate_sb[:, FILL], MULT)
+        nc.vector.tensor_copy(y[1][:, FILL.stop : LEAD.stop], lead_other[:, FILL.stop :])
         gated_on_vector(MID, mid)
         nc.scalar.activation(y[1][:, MID], mid_other, COPY)
         scatter_on_scalar(MID)
@@ -193,10 +199,10 @@ def tile_picked_route2_linnone_e_kernel(tc, xT, gate, w1_words, w1_scales, offs,
         end_other = multiply(1, pieces(5, 7), piece(7))
         end = multiply(0, pieces(5, 7), piece(7))
 
-        scatter_on_vector(LEAD)
+        nc.vector.tensor_tensor(window[1][:].indirect(entries(place, FILL)), y[1][:, FILL], zeros[:], ADD)
         nc.vector.tensor_copy(y[1][:, END], end_other)
         gated_on_vector(END, end)
         scatter_on_scalar(END)
-        scatter_on_vector(slice(LEAD.stop, S))
+        scatter_on_vector(slice(FILL.stop, S))
         for b in range(2):
             nc.sync.dma_start(out=out[P * b : P * (b + 1), :], in_=window[b][:])

@@ -138,9 +138,14 @@ def tile_picked_route2_linnone_e_kernel(tc, xT, gate, w1_words, w1_scales, offs,
                 in_=woven[:, PACK * part.start : PACK * part.stop],
             )
 
+        def bank(b, span):
+            return psum.tile([P, width(span)], F32, name=f"acc{span.start}_{b}")
+
         def multiply(b, *parts):
-            first = parts[0].start
-            acc = psum.tile([P, parts[-1].stop - first], F32, name=f"acc{first}_{b}")
+            span = slice(parts[0].start, parts[-1].stop)
+            return multiply_into(bank(b, span), span.start, b, *parts)
+
+        def multiply_into(acc, first, b, *parts):
             for part in parts:
                 nc.tensor.matmul_mx(
                     out=acc[:, part.start - first : part.stop - first],
@@ -163,13 +168,11 @@ def tile_picked_route2_linnone_e_kernel(tc, xT, gate, w1_words, w1_scales, offs,
             nc.vector.tensor_tensor(window[1][:].indirect(entries(place, part)), y[1][:, part], gate_sb[:, part], MULT)
 
         fetch_on_vector(piece(0))
-        fetch_on_vector(piece(2))
-        fetch_on_scalar(piece(1))
+        fetch_on_vector(piece(1))
         nc.scalar.activation(pair[:, 1, :], source(last, PAIRED), COPY)
-        fetch_on_scalar(piece(3))
-        fetch_on_scalar(piece(5))
+        fetch_on_scalar(pieces(2, 4))
         nc.scalar.activation(picked[:, PAIRED, last - 1 :], pair[:].rearrange("p j n -> p n j"), COPY)
-        fetch_on_scalar(pieces(6, 8))
+        fetch_on_scalar(LATE)
 
         new_codes(LEAD, "lead_codes")
         weave(piece(0))
@@ -185,22 +188,27 @@ def tile_picked_route2_linnone_e_kernel(tc, xT, gate, w1_words, w1_scales, offs,
         scatter_on_scalar(LEAD)
 
         new_codes(MID, "later_codes")
-        quantise(MID)
-        mid = multiply(0, pieces(2, 4), piece(4))
-        mid_other = multiply(1, pieces(2, 4), piece(4))
+        quantise(PAIRED)
+        quantise(pieces(2, 4))
+        mid = bank(0, MID)
+        multiply_into(mid, MID.start, 0, PAIRED, pieces(2, 4))
+        mid_other = multiply(1, pieces(2, 4))
+        rest = pieces(4, 8)
+        rest_other = bank(1, rest)
+        multiply_into(rest_other, rest.start, 1, piece(4))
         weave(LATE)
         nc.vector.tensor_tensor(y[1][:, FILL], lead_other[:, FILL], gate_sb[:, FILL], MULT)
         nc.vector.tensor_copy(y[1][:, FILL.stop : LEAD.stop], lead_other[:, FILL.stop :])
-        gated_on_vector(MID, mid)
-        nc.scalar.activation(y[1][:, MID], mid_other, COPY)
+        gated_on_vector(MID, mid[:])
+        nc.scalar.activation(y[1][:, pieces(2, 4)], mid_other, COPY)
         scatter_on_scalar(MID)
         new_codes(END, "later_codes")
         quantise(END)
-        end_other = multiply(1, pieces(5, 7), piece(7))
+        multiply_into(rest_other, rest.start, 1, pieces(5, 7), piece(7))
         end = multiply(0, pieces(5, 7), piece(7))
 
         nc.vector.tensor_tensor(window[1][:].indirect(entries(place, FILL)), y[1][:, FILL], zeros[:], ADD)
-        nc.vector.tensor_copy(y[1][:, END], end_other)
+        nc.vector.tensor_copy(y[1][:, rest], rest_other[:])
         gated_on_vector(END, end)
         scatter_on_scalar(END)
         scatter_on_vector(slice(FILL.stop, S))

@@ -39,7 +39,7 @@ def width(part):
 
 LEAD, MID, END = pieces(0, 2), pieces(2, 5), pieces(5, 8)
 FILL = slice(0, 3 * PIECE // 2)
-EARLY, PAIRED, LATE = pieces(0, 4), piece(4), END
+EARLY, PAIRED, LATE = pieces(0, 4), pieces(4, 6), pieces(6, 8)
 
 
 def tile_picked_route2_linnone_e_kernel(tc, xT, gate, w1_words, w1_scales, offs, dst, out):
@@ -171,8 +171,10 @@ def tile_picked_route2_linnone_e_kernel(tc, xT, gate, w1_words, w1_scales, offs,
         fetch_on_vector(piece(1))
         nc.scalar.activation(pair[:, 1, :], source(last, PAIRED), COPY)
         fetch_on_scalar(pieces(2, 4))
-        nc.scalar.activation(picked[:, PAIRED, last - 1 :], pair[:].rearrange("p j n -> p n j"), COPY)
+        pairs = pair[:].rearrange("p j n -> p n j")
+        nc.scalar.activation(picked[:, piece(4), last - 1 :], pairs[:, piece(0), :], COPY)
         fetch_on_scalar(LATE)
+        nc.scalar.activation(picked[:, piece(5), last - 1 :], pairs[:, piece(1), :], COPY)
 
         new_codes(LEAD, "lead_codes")
         weave(piece(0))
@@ -188,10 +190,10 @@ def tile_picked_route2_linnone_e_kernel(tc, xT, gate, w1_words, w1_scales, offs,
         scatter_on_scalar(LEAD)
 
         new_codes(MID, "later_codes")
-        quantise(PAIRED)
+        quantise(piece(4))
         quantise(pieces(2, 4))
         mid = bank(0, MID)
-        multiply_into(mid, MID.start, 0, PAIRED, pieces(2, 4))
+        multiply_into(mid, MID.start, 0, piece(4), pieces(2, 4))
         mid_other = multiply(1, pieces(2, 4))
         rest = pieces(4, 8)
         rest_other = bank(1, rest)

@@ -76,17 +76,17 @@ def tile_picked_route2_linnone_e_kernel(tc, xT, gate, w1_words, w1_scales, offs,
         nc.sync.dma_start(pick[:], offs)
         nc.vector.memset(w_scales[:].bitcast(I32), 0)
         for q in range(4):
-            nc.sync.dma_start(
+            nc.scalar.dma_start(
                 out=w_scales[32 * q : 32 * q + 4, :].bitcast(I32),
                 in_=w1_scales[0, 4 * q : 4 * q + 4, :].bitcast(I32),
             )
-        nc.sync.dma_start(out=plane[1][:], in_=x_planes[:, 1, :])
-        nc.sync.dma_start(place[:], dst)
-        for j in range(2, PACK):
+        for j in range(1, PACK):
             nc.sync.dma_start(out=plane[j][:], in_=x_planes[:, j, :])
         for b in range(2):
             cols = slice(2 * P * b, 2 * P * (b + 1))
             nc.sync.dma_start(out=w_codes[:, cols].bitcast(I32), in_=w1_words[0][:, cols].bitcast(I32))
+            if b == 0:
+                nc.sync.dma_start(place[:], dst)
 
         for b in range(2):
             nc.vector.memset(window[b][:], 0.0)

@@ -15,7 +15,6 @@ FP8X4 = mybir.dt.float8_e4m3fn_x4
 FP4X4 = mybir.dt.float4_e2m1fn_x4
 COPY = mybir.ActivationFunctionType.Copy
 MULT = mybir.AluOpType.mult
-ADD = mybir.AluOpType.add
 
 P = 128
 PACK = 4
@@ -29,17 +28,11 @@ def pieces(first, stop):
     return slice(first * PIECE, stop * PIECE)
 
 
-def piece(i):
-    return pieces(i, i + 1)
-
-
 def width(part):
     return part.stop - part.start
 
 
-LEAD, MID, END = pieces(0, 2), pieces(2, 5), pieces(5, 8)
-FILL = slice(0, 3 * PIECE // 2)
-EARLY, PAIRED, LATE = pieces(0, 4), pieces(4, 6), pieces(6, 8)
+LEAD, LAST, OWN, THIRD = pieces(0, 2), pieces(2, 4), pieces(4, 6), pieces(6, 8)
 
 
 def tile_picked_route2_linnone_e_kernel(tc, xT, gate, w1_words, w1_scales, offs, dst, out):
@@ -58,14 +51,15 @@ def tile_picked_route2_linnone_e_kernel(tc, xT, gate, w1_words, w1_scales, offs,
         plane = [tile(f"plane{j}", [P, T], F32) for j in range(PACK)]
         woven = tile("woven", [P, S * PACK], BF16)
         picked = woven[:].rearrange("p (n j) -> p n j", j=PACK)
+        codes = tile("codes", [P, S], U32)
         scales = tile("scales", [P, S], U8)
         w_codes = tile("w_codes", [P, 2 * N], U8)
         w_scales = tile("w_scales", [P, N], U8)
         gate_sb = tile("gate_sb", [P, S], F32)
         y = [tile(f"y{b}", [P, S], F32) for b in range(2)]
         window = [tile(f"window{b}", [P, U], F32) for b in range(2)]
+        one = tile("one", [P, 1], F32)
         plain = tile("plain", [P, S], BF16)
-        pair = tile("pair", [P, 2, width(PAIRED)], BF16)
 
         def entries(list_tile, part):
             return list_tile[:, part.start // STRIPE : part.stop // STRIPE]
@@ -90,8 +84,7 @@ def tile_picked_route2_linnone_e_kernel(tc, xT, gate, w1_words, w1_scales, offs,
 
         for b in range(2):
             nc.vector.memset(window[b][:], 0.0)
-        zeros = tile("zeros", [P, width(FILL)], F32)
-        nc.vector.memset(zeros[:], 0.0)
+        nc.vector.memset(one[:], 1.0)
 
         gate_turned = tile("gate_turned", [P, SQUARE], F32)
         nc.vector.transpose(gate_turned[:], gate_rows[:])
@@ -101,39 +94,21 @@ def tile_picked_route2_linnone_e_kernel(tc, xT, gate, w1_words, w1_scales, offs,
 
         last = PACK - 1
 
-        def source(j, part):
-            return plane[j][:].indirect(entries(pick, part))
+        def fetch_on_vector(j, part):
+            nc.vector.tensor_copy(picked[:, part, j], plane[j][:].indirect(entries(pick, part)))
 
-        for j in range(last - 1):
-            nc.vector.tensor_copy(picked[:, :, j], source(j, slice(0, S)))
-        nc.vector.tensor_copy(picked[:, EARLY, last - 1], source(last - 1, EARLY))
-        nc.scalar.activation(plain[:, LATE], source(last - 1, LATE), COPY)
-        nc.scalar.activation(pair[:, 0, :], source(last - 1, PAIRED), COPY)
-        nc.vector.tensor_copy(picked[:, LATE, last - 1], plain[:, LATE])
+        def fetch_on_scalar(j, part):
+            nc.scalar.activation(picked[:, part, j], plane[j][:].indirect(entries(pick, part)), COPY)
 
-        def fetch_on_vector(part):
-            nc.vector.tensor_copy(plain[:, part], source(last, part))
+        def fetch_plainly(j, part):
+            nc.vector.tensor_copy(plain[:, part], plane[j][:].indirect(entries(pick, part)))
 
-        def fetch_on_scalar(part):
-            nc.scalar.activation(plain[:, part], source(last, part), COPY)
-
-        def weave(part):
-            nc.vector.tensor_copy(picked[:, part, last], plain[:, part])
-
-        codes = {}
-
-        def new_codes(part, tag):
-            made = keep.tile([P, width(part)], U32, name=f"codes{part.start}", tag=tag, align_bytes=ALIGN)
-            for i in range(part.start // PIECE, part.stop // PIECE):
-                codes[i] = (made, part.start)
-
-        def codes_of(part):
-            made, first = codes[part.start // PIECE]
-            return made[:, part.start - first : part.stop - first].bitcast(FP8X4)
+        def weave(j, part):
+            nc.vector.tensor_copy(picked[:, part, j], plain[:, part])
 
         def quantise(part):
             nc.vector.quantize_mx(
-                out=codes_of(part),
+                out=codes[:, part].bitcast(FP8X4),
                 scales=scales[:, part],
                 in_=woven[:, PACK * part.start : PACK * part.stop],
             )
@@ -141,78 +116,68 @@ def tile_picked_route2_linnone_e_kernel(tc, xT, gate, w1_words, w1_scales, offs,
         def bank(b, span):
             return psum.tile([P, width(span)], F32, name=f"acc{span.start}_{b}")
 
-        def multiply(b, *parts):
-            span = slice(parts[0].start, parts[-1].stop)
-            return multiply_into(bank(b, span), span.start, b, *parts)
-
         def multiply_into(acc, first, b, *parts):
             for part in parts:
                 nc.tensor.matmul_mx(
                     out=acc[:, part.start - first : part.stop - first],
                     lhsT=w_codes[:, 2 * P * b : 2 * P * (b + 1)].bitcast(FP4X4),
                     lhsT_scale=w_scales[:, P * b : P * (b + 1)],
-                    rhs=codes_of(part),
+                    rhs=codes[:, part].bitcast(FP8X4),
                     rhs_scale=scales[:, part],
                     start=True,
                     stop=True,
                 )
             return acc[:]
 
+        def multiply(b, *parts):
+            span = slice(parts[0].start, parts[-1].stop)
+            return multiply_into(bank(b, span), span.start, b, *parts)
+
         def gated_on_vector(part, acc):
             nc.vector.tensor_tensor(y[0][:, part], acc, gate_sb[:, part], MULT)
 
         def scatter_on_scalar(part):
-            nc.scalar.activation(window[0][:].indirect(entries(place, part)), y[0][:, part], COPY)
+            nc.scalar.activation(window[0][:].indirect(entries(place, part)), y[0][:, part], COPY, scale=one[:])
 
         def scatter_on_vector(part):
             nc.vector.tensor_tensor(window[1][:].indirect(entries(place, part)), y[1][:, part], gate_sb[:, part], MULT)
 
-        fetch_on_vector(piece(0))
-        fetch_on_vector(piece(1))
-        nc.scalar.activation(pair[:, 1, :], source(last, PAIRED), COPY)
-        fetch_on_scalar(pieces(2, 4))
-        pairs = pair[:].rearrange("p j n -> p n j")
-        nc.scalar.activation(picked[:, piece(4), last - 1 :], pairs[:, piece(0), :], COPY)
-        fetch_on_scalar(LATE)
-        nc.scalar.activation(picked[:, piece(5), last - 1 :], pairs[:, piece(1), :], COPY)
+        for j in range(last - 1):
+            fetch_on_vector(j, slice(0, S))
+        fetch_on_scalar(last - 1, slice(LEAD.start, LAST.stop))
+        fetch_on_scalar(last - 1, THIRD)
+        fetch_plainly(last - 1, OWN)
+        weave(last - 1, OWN)
 
-        new_codes(LEAD, "lead_codes")
-        weave(piece(0))
-        weave(piece(1))
-        lead = []
-        for i in range(2):
-            quantise(piece(i))
-            lead.append(multiply(0, piece(i)))
+        for part in (LEAD, THIRD, LAST):
+            fetch_on_scalar(last, part)
+        own = [pieces(4, 5), pieces(5, 6)]
+        for part in own:
+            fetch_plainly(last, part)
+        for part in own:
+            weave(last, part)
+
+        quantise(LEAD)
+        lead = multiply(0, LEAD)
+        quantise(OWN)
+        quantise(THIRD)
+        back = slice(OWN.start, THIRD.stop)
+        mid = multiply(0, back)
+        third_other = multiply(1, THIRD)
         lead_other = multiply(1, LEAD)
-        weave(pieces(2, 4))
-        for i in range(2):
-            gated_on_vector(piece(i), lead[i])
+        gated_on_vector(LEAD, lead)
         scatter_on_scalar(LEAD)
+        quantise(LAST)
+        end = multiply(0, LAST)
+        inner = slice(LAST.start, OWN.stop)
+        inner_other = multiply(1, inner)
+        gated_on_vector(back, mid)
+        nc.vector.tensor_copy(y[1][:, LEAD], lead_other)
+        gated_on_vector(LAST, end)
+        nc.scalar.activation(y[1][:, THIRD], third_other, COPY)
+        scatter_on_scalar(slice(LAST.start, S))
+        nc.vector.tensor_copy(y[1][:, inner], inner_other)
+        scatter_on_vector(slice(0, S))
 
-        new_codes(MID, "later_codes")
-        quantise(piece(4))
-        quantise(pieces(2, 4))
-        mid = bank(0, MID)
-        multiply_into(mid, MID.start, 0, piece(4), pieces(2, 4))
-        mid_other = multiply(1, pieces(2, 4))
-        rest = pieces(4, 8)
-        rest_other = bank(1, rest)
-        multiply_into(rest_other, rest.start, 1, piece(4))
-        weave(LATE)
-        nc.vector.tensor_tensor(y[1][:, FILL], lead_other[:, FILL], gate_sb[:, FILL], MULT)
-        nc.vector.tensor_copy(y[1][:, FILL.stop : LEAD.stop], lead_other[:, FILL.stop :])
-        gated_on_vector(MID, mid[:])
-        nc.scalar.activation(y[1][:, pieces(2, 4)], mid_other, COPY)
-        scatter_on_scalar(MID)
-        new_codes(END, "later_codes")
-        quantise(END)
-        multiply_into(rest_other, rest.start, 1, pieces(5, 7), piece(7))
-        end = multiply(0, pieces(5, 7), piece(7))
-
-        nc.vector.tensor_tensor(window[1][:].indirect(entries(place, FILL)), y[1][:, FILL], zeros[:], ADD)
-        nc.vector.tensor_copy(y[1][:, rest], rest_other[:])
-        gated_on_vector(END, end)
-        scatter_on_scalar(END)
-        scatter_on_vector(slice(FILL.stop, S))
         for b in range(2):
             nc.sync.dma_start(out=out[P * b : P * (b + 1), :], in_=window[b][:])

@@ -32,7 +32,8 @@ def width(part):
     return part.stop - part.start
 
 
-LEAD, LAST, OWN, THIRD = pieces(0, 2), pieces(2, 4), pieces(4, 6), pieces(6, 8)
+LEAD, MID, END = pieces(0, 2), pieces(2, 5), pieces(5, 8)
+OWN = pieces(1, 3)
 
 
 def tile_picked_route2_linnone_e_kernel(tc, xT, gate, w1_words, w1_scales, offs, dst, out):
@@ -144,39 +145,41 @@ def tile_picked_route2_linnone_e_kernel(tc, xT, gate, w1_words, w1_scales, offs,
 
         for j in range(last - 1):
             fetch_on_vector(j, slice(0, S))
-        fetch_on_scalar(last - 1, slice(LEAD.start, LAST.stop))
-        fetch_on_scalar(last - 1, THIRD)
+        fetch_on_scalar(last - 1, pieces(0, 1))
+        fetch_on_scalar(last - 1, pieces(3, 8))
         fetch_plainly(last - 1, OWN)
         weave(last - 1, OWN)
 
-        for part in (LEAD, THIRD, LAST):
+        for part in (pieces(0, 1), pieces(3, 5), pieces(5, 7), pieces(7, 8)):
             fetch_on_scalar(last, part)
-        own = [pieces(4, 5), pieces(5, 6)]
+        own = [pieces(1, 2), pieces(2, 3)]
         for part in own:
             fetch_plainly(last, part)
         for part in own:
             weave(last, part)
 
-        quantise(LEAD)
-        lead = multiply(0, LEAD)
-        quantise(OWN)
-        quantise(THIRD)
-        back = slice(OWN.start, THIRD.stop)
-        mid = multiply(0, back)
-        third_other = multiply(1, THIRD)
-        lead_other = multiply(1, LEAD)
-        gated_on_vector(LEAD, lead)
+        first = [pieces(0, 1), pieces(1, 2)]
+        lead = []
+        for part in first:
+            quantise(part)
+            lead.append(multiply(0, part))
+        quantise(MID)
+        mid = multiply(0, pieces(2, 4), pieces(4, 5))
+        front_other = multiply(1, pieces(0, 2), pieces(2, 3))
+        for part, acc in zip(first, lead):
+            gated_on_vector(part, acc)
         scatter_on_scalar(LEAD)
-        quantise(LAST)
-        end = multiply(0, LAST)
-        inner = slice(LAST.start, OWN.stop)
-        inner_other = multiply(1, inner)
-        gated_on_vector(back, mid)
-        nc.vector.tensor_copy(y[1][:, LEAD], lead_other)
-        gated_on_vector(LAST, end)
-        nc.scalar.activation(y[1][:, THIRD], third_other, COPY)
-        scatter_on_scalar(slice(LAST.start, S))
-        nc.vector.tensor_copy(y[1][:, inner], inner_other)
+        quantise(pieces(5, 7))
+        quantise(pieces(7, 8))
+        end = multiply(0, pieces(5, 7), pieces(7, 8))
+        end_other = multiply(1, pieces(6, 8))
+        inner_other = multiply(1, pieces(3, 4), pieces(4, 6))
+        gated_on_vector(MID, mid)
+        nc.vector.tensor_copy(y[1][:, pieces(0, 3)], front_other)
+        gated_on_vector(END, end)
+        nc.scalar.activation(y[1][:, pieces(6, 8)], end_other, COPY)
+        scatter_on_scalar(slice(MID.start, S))
+        nc.vector.tensor_copy(y[1][:, pieces(3, 6)], inner_other)
         scatter_on_vector(slice(0, S))
 
         for b in range(2):

@@ -67,7 +67,10 @@ def tile_picked_route2_linnone_e_kernel(tc, xT, gate, w1_words, w1_scales, offs,
 
         nc.sync.dma_start(out=plane[0][:], in_=x_planes[:, 0, :])
         gate_rows = tile("gate_rows", [P, SQUARE], F32)
-        nc.scalar.dma_start(out=gate_rows[:], in_=gate[0 : P * SQUARE // S, :].rearrange("r (i c) -> (r i) c", c=SQUARE))
+        gate_cut = gate[0 : P * SQUARE // S, :].rearrange("r (i c) -> (r i) c", c=SQUARE)
+        for half in (slice(0, P // 2), slice(P // 2, P)):
+            nc.scalar.dma_start(out=gate_rows[half, :], in_=gate_cut[half, :])
+        nc.sync.dma_start(out=plane[1][:], in_=x_planes[:, 1, :])
         nc.sync.dma_start(pick[:], offs)
         nc.vector.memset(w_scales[:].bitcast(I32), 0)
         for q in range(4):
@@ -75,7 +78,7 @@ def tile_picked_route2_linnone_e_kernel(tc, xT, gate, w1_words, w1_scales, offs,
                 out=w_scales[32 * q : 32 * q + 4, :].bitcast(I32),
                 in_=w1_scales[0, 4 * q : 4 * q + 4, :].bitcast(I32),
             )
-        for j in range(1, PACK):
+        for j in range(2, PACK):
             nc.sync.dma_start(out=plane[j][:], in_=x_planes[:, j, :])
         for b in range(2):
             cols = slice(2 * P * b, 2 * P * (b + 1))
@@ -144,7 +147,8 @@ def tile_picked_route2_linnone_e_kernel(tc, xT, gate, w1_words, w1_scales, offs,
             nc.vector.tensor_tensor(window[1][:].indirect(entries(place, part)), y[1][:, part], gate_sb[:, part], MULT)
 
         for j in range(last - 1):
-            fetch_on_vector(j, slice(0, S))
+            fetch_on_vector(j, pieces(0, 5))
+            fetch_on_scalar(j, pieces(5, 8))
         fetch_on_scalar(last - 1, pieces(0, 1))
         fetch_on_scalar(last - 1, pieces(3, 8))
         fetch_plainly(last - 1, OWN)

from contextlib import ExitStack

import concourse.mybir as mybir

K, T, S, N, U = 512, 4096, 1024, 256, 2048
FLOPS = 2 * K * N * S

F32 = mybir.dt.float32
BF16 = mybir.dt.bfloat16
I32 = mybir.dt.int32
U32 = mybir.dt.uint32
U16 = mybir.dt.uint16
U8 = mybir.dt.uint8
FP8X4 = mybir.dt.float8_e4m3fn_x4
FP4X4 = mybir.dt.float4_e2m1fn_x4
COPY = mybir.ActivationFunctionType.Copy
MULT = mybir.AluOpType.mult

P = 128
PACK = 4
STRIPE = 16
ALIGN = 256
PIECE = 128
SQUARE = 32


def pieces(first, stop):
    return slice(first * PIECE, stop * PIECE)


def width(part):
    return part.stop - part.start


LEAD, MID, END = pieces(0, 2), pieces(2, 5), pieces(5, 8)
OWN = pieces(1, 3)


def tile_picked_route2_linnone_e_kernel(tc, xT, gate, w1_words, w1_scales, offs, dst, out):
    nc = tc.nc
    x_planes = xT.rearrange("(p j) t -> p j t", j=PACK)

    with ExitStack() as ctx:
        keep = ctx.enter_context(tc.tile_pool(name="keep", bufs=1))
        psum = ctx.enter_context(tc.psum_pool(name="psum", bufs=1))

        def tile(name, shape, dtype):
            return keep.tile(shape, dtype, name=name, align_bytes=ALIGN)

        pick = tile("pick", [P, S // STRIPE], U16)
        place = tile("place", [P, S // STRIPE], U16)
        plane = [tile(f"plane{j}", [P, T], F32) for j in range(PACK)]
        woven = tile("woven", [P, S * PACK], BF16)
        picked = woven[:].rearrange("p (n j) -> p n j", j=PACK)
        codes = tile("codes", [P, S], U32)
        scales = tile("scales", [P, S], U8)
        w_codes = tile("w_codes", [P, 2 * N], U8)
        w_scales = tile("w_scales", [P, N], U8)
        gate_sb = tile("gate_sb", [P, S], F32)
        y = [tile(f"y{b}", [P, S], F32) for b in range(2)]
        window = [tile(f"window{b}", [P, U], F32) for b in range(2)]
        one = tile("one", [P, 1], F32)
        plain = tile("plain", [P, S], BF16)

        def entries(list_tile, part):
            return list_tile[:, part.start // STRIPE : part.stop // STRIPE]

        nc.sync.dma_start(out=plane[0][:], in_=x_planes[:, 0, :])
        gate_rows = tile("gate_rows", [P, SQUARE], F32)
        gate_cut = gate[0 : P * SQUARE // S, :].rearrange("r (i c) -> (r i) c", c=SQUARE)
        for half in (slice(0, P // 2), slice(P // 2, P)):
            nc.scalar.dma_start(out=gate_rows[half, :], in_=gate_cut[half, :])
        nc.sync.dma_start(out=plane[1][:], in_=x_planes[:, 1, :])
        nc.sync.dma_start(pick[:], offs)
        nc.vector.memset(w_scales[:].bitcast(I32), 0)
        for q in range(4):
            nc.scalar.dma_start(
                out=w_scales[32 * q : 32 * q + 4, :].bitcast(I32),
                in_=w1_scales[0, 4 * q : 4 * q + 4, :].bitcast(I32),
            )
        for j in range(2, PACK):
            nc.sync.dma_start(out=plane[j][:], in_=x_planes[:, j, :])
        for b in range(2):
            cols = slice(2 * P * b, 2 * P * (b + 1))
            nc.sync.dma_start(out=w_codes[:, cols].bitcast(I32), in_=w1_words[0][:, cols].bitcast(I32))
            if b == 0:
                nc.sync.dma_start(place[:], dst)

        for b in range(2):
            nc.vector.memset(window[b][:], 0.0)
        nc.vector.memset(one[:], 1.0)

        gate_turned = tile("gate_turned", [P, SQUARE], F32)
        nc.vector.transpose(gate_turned[:], gate_rows[:])
        gate_spread = tile("gate_spread", [P, SQUARE, SQUARE], F32)
        nc.scalar.activation(gate_spread[:], gate_turned[:].unsqueeze(2).to_broadcast([P, SQUARE, SQUARE]), COPY)
        nc.vector.transpose(gate_sb[:], gate_spread[:].rearrange("p b r -> p (b r)"))

        last = PACK - 1

        def fetch_on_vector(j, part):
            nc.vector.tensor_copy(picked[:, part, j], plane[j][:].indirect(entries(pick, part)))

        def fetch_on_scalar(j, part):
            nc.scalar.activation(picked[:, part, j], plane[j][:].indirect(entries(pick, part)), COPY)

        def fetch_plainly(j, part):
            nc.vector.tensor_copy(plain[:, part], plane[j][:].indirect(entries(pick, part)))

        def weave(j, part):
            nc.vector.tensor_copy(picked[:, part, j], plain[:, part])

        def quantise(part):
            nc.vector.quantize_mx(
                out=codes[:, part].bitcast(FP8X4),
                scales=scales[:, part],
                in_=woven[:, PACK * part.start : PACK * part.stop],
            )

        def bank(b, span):
            return psum.tile([P, width(span)], F32, name=f"acc{span.start}_{b}")

        def multiply_into(acc, first, b, *parts):
            for part in parts:
                nc.tensor.matmul_mx(
                    out=acc[:, part.start - first : part.stop - first],
                    lhsT=w_codes[:, 2 * P * b : 2 * P * (b + 1)].bitcast(FP4X4),
                    lhsT_scale=w_scales[:, P * b : P * (b + 1)],
                    rhs=codes[:, part].bitcast(FP8X4),
                    rhs_scale=scales[:, part],
                    start=True,
                    stop=True,
                )
            return acc[:]

        def multiply(b, *parts):
            span = slice(parts[0].start, parts[-1].stop)
            return multiply_into(bank(b, span), span.start, b, *parts)

        def gated_on_vector(part, acc):
            nc.vector.tensor_tensor(y[0][:, part], acc, gate_sb[:, part], MULT)

        def scatter_on_scalar(part):
            nc.scalar.activation(window[0][:].indirect(entries(place, part)), y[0][:, part], COPY, scale=one[:])

        def scatter_on_vector(part):
            nc.vector.tensor_tensor(window[1][:].indirect(entries(place, part)), y[1][:, part], gate_sb[:, part], MULT)

        for j in range(last - 1):
            fetch_on_vector(j, pieces(0, 5))
            fetch_on_scalar(j, pieces(5, 8))
        fetch_on_scalar(last - 1, pieces(0, 1))
        fetch_on_scalar(last - 1, pieces(3, 8))
        fetch_plainly(last - 1, OWN)
        weave(last - 1, OWN)

        for part in (pieces(0, 1), pieces(3, 5), pieces(5, 7), pieces(7, 8)):
            fetch_on_scalar(last, part)
        own = [pieces(1, 2), pieces(2, 3)]
        for part in own:
            fetch_plainly(last, part)
        for part in own:
            weave(last, part)

        first = [pieces(0, 1), pieces(1, 2)]
        lead = []
        for part in first:
            quantise(part)
            lead.append(multiply(0, part))
        quantise(MID)
        mid = multiply(0, pieces(2, 4), pieces(4, 5))
        front_other = multiply(1, pieces(0, 2), pieces(2, 3))
        for part, acc in zip(first, lead):
            gated_on_vector(part, acc)
        scatter_on_scalar(LEAD)
        quantise(pieces(5, 7))
        quantise(pieces(7, 8))
        end = multiply(0, pieces(5, 7), pieces(7, 8))
        end_other = multiply(1, pieces(6, 8))
        inner_other = multiply(1, pieces(3, 4), pieces(4, 6))
        gated_on_vector(MID, mid)
        nc.vector.tensor_copy(y[1][:, pieces(0, 3)], front_other)
        gated_on_vector(END, end)
        nc.scalar.activation(y[1][:, pieces(6, 8)], end_other, COPY)
        scatter_on_scalar(slice(MID.start, S))
        nc.vector.tensor_copy(y[1][:, pieces(3, 6)], inner_other)
        scatter_on_vector(slice(0, S))

        for b in range(2):
            nc.sync.dma_start(out=out[P * b : P * (b + 1), :], in_=window[b][:])
